import numpy as np
import ml_dtypes


def mxq(x, axis, fmt="e4m3"):
    dtype, down = {"e4m3": (ml_dtypes.float8_e4m3fn, 7), "e5m2": (ml_dtypes.float8_e5m2, 14)}[fmt]
    v = np.moveaxis(np.asarray(x, np.float32).astype(ml_dtypes.bfloat16).astype(np.float64), axis, -1)
    blocks = v.reshape(v.shape[:-1] + (-1, 32))
    amax = np.abs(blocks).max(-1, keepdims=True)
    byte = np.maximum(np.where(amax > 0, np.frexp(amax)[1] - 1 + 127, 0) - down, 1)
    scale = np.exp2(byte - 127.0)
    codes = (blocks / scale).astype(np.float32).astype(dtype).astype(np.float64)
    return np.moveaxis((codes * scale).reshape(v.shape), -1, axis)


WIDE = False


def mx_kscale(k):
    if not WIDE:
        return np.ones(k)
    levels = np.array([10, -10, 5, -5, 0])
    if k % 512:
        return np.exp2(np.random.permutation(np.resize(levels, k // 32))).repeat(32)
    a = np.empty((k // 512, 16))
    for p in range(k // 512):
        a[p, :8] = np.random.permutation(np.resize(levels, 8))
        for g in range(8):
            far = levels[np.abs(levels - a[p, g]) >= 10]
            a[p, g + 8] = far[np.random.randint(len(far))]
    return np.exp2(a.ravel()).repeat(32)


def f64(x):
    return np.asarray(x).astype(np.float64)


def striped(idx):
    return np.tile(idx.reshape(-1, 16).T, (8, 1)).astype(np.uint16)


def unstriped(offs):
    return offs[:16].T.reshape(-1).astype(np.int64)


E2M1 = np.array([0.0, 0.5, 1.0, 1.5, 2.0, 3.0, 4.0, 6.0, -0.0, -0.5, -1.0, -1.5, -2.0, -3.0, -4.0, -6.0])


def pack_weight(w, fmt):
    k, n = w.shape
    w = f64(np.asarray(w, np.float32).astype(ml_dtypes.bfloat16)).reshape(k // 32, 32, n)
    amax = np.abs(w).max(1)
    if fmt == "e4m3":
        byte = np.frexp(amax)[1] - 1 + 127 - 7
    else:
        mant, ex = np.frexp(amax / 6.0)
        byte = np.where(mant > 0.5, ex, ex - 1) + 127
    byte = np.clip(np.where(amax > 0, byte, 1), 1, 254)
    scaled = (w * np.exp2(127.0 - byte)[:, None, :]).reshape(k, n).astype(np.float32)
    by_word = np.ascontiguousarray(scaled.reshape(k // 512, 128, 4, n).transpose(0, 1, 3, 2))
    if fmt == "e4m3":
        words = by_word.astype(ml_dtypes.float8_e4m3fn).view(np.uint8)
    else:
        c = by_word.astype(ml_dtypes.float4_e2m1fn).view(np.uint8) & 0xF
        words = (c[..., 0::2] | (c[..., 1::2] << 4)).reshape(k // 512, 128, 2 * n)
    return np.ascontiguousarray(words), np.ascontiguousarray(byte.astype(np.uint8).reshape(k // 512, 16, n))


def unpack_weight(words, scales, fmt):
    g, _, n = scales.shape
    words = np.ascontiguousarray(words).reshape(g, 128, n, -1)
    if fmt == "e4m3":
        vals = words.view(ml_dtypes.float8_e4m3fn).astype(np.float64)
    else:
        nib = np.empty((g, 128, n, 4), np.uint8)
        nib[..., 0::2] = words & 0xF
        nib[..., 1::2] = words >> 4
        vals = E2M1[nib]
    vals = vals * np.repeat(np.exp2(scales.astype(np.float64) - 127.0), 8, axis=1)[..., None]
    return vals.transpose(0, 1, 3, 2).reshape(g * 512, n)


def gelu(v):
    return 0.5 * v * (1.0 + np.tanh(np.sqrt(2.0 / np.pi) * (v + 0.044715 * v**3)))


K, K2, H, N, T, S, T3, P = 1024, 512, 1024, 512, 4096, 1024, 2048, 512

def setup_inputs():
    n = np.random.standard_normal
    s, s2, u = mx_kscale(K)[:, None], mx_kscale(K2)[:, None], mx_kscale(H)[:, None]
    d = {}
    d["tab_words"], d["tab_scales"] = pack_weight(n((K, T)) * s, "e4m3")
    d["tab2_words"], d["tab2_scales"] = pack_weight(n((K2, T3)) * s2, "e4m3")
    d["offs"] = striped(np.random.permutation(T)[:S])
    d["offs2"] = striped(np.random.permutation(T3)[:P])
    d["pos1"] = striped(np.random.permutation(S)[:P])
    d["w1_words"], d["w1_scales"] = pack_weight(n((K, H)) / K ** 0.5 / s * u.T, "e2m1")
    d["cap"] = ((0.3 + 0.5 * n(H)) * u[:, 0]).astype(np.float32)
    d["w2"] = (0.35 * n((K2, H)) / K2 ** 0.5 / s2).astype(np.float32)
    d["w3_words"], d["w3_scales"] = pack_weight(0.55 * n((K2, H)) / K2 ** 0.5 / s2, "e4m3")
    d["wgs"] = np.exp(0.3 * n((128, P))).astype(np.float32)
    d["gm"] = (2.5 * n((H, S)) * u).astype(np.float32)
    d["w4"] = (n((H, N)) / H ** 0.5 / u).astype(np.float32)
    return d

def reference(tab_words, tab_scales, tab2_words, tab2_scales, offs, offs2, pos1, w1_words, w1_scales, cap, w2, w3_words, w3_scales, wgs, gm, w4):
    v = unpack_weight(tab_words, tab_scales, "e4m3")[:, unstriped(offs)]
    v2 = unpack_weight(tab2_words, tab2_scales, "e4m3")[:, unstriped(offs2)]
    a = np.minimum(unpack_weight(w1_words, w1_scales, "e2m1").T @ v, f64(cap)[:, None])
    lin = mxq(f64(w2), 0, "e4m3").T @ v2
    b = lin + np.sin(unpack_weight(w3_words, w3_scales, "e4m3").T @ v2)
    placed = np.zeros((H, S))
    placed[:, unstriped(pos1)] = np.tile(f64(wgs), (H // 128, 1)) * b
    z = a + placed * f64(gm)
    return mxq(f64(w4), 0, "e4m3").T @ mxq(z, 0, "e4m3")

@@ -1,0 +1,313 @@
+import math
+from contextlib import ExitStack
+
+import concourse.mybir as mybir
+
+K, K2, H, N, T, S, T3, P = 1024, 512, 1024, 512, 4096, 1024, 2048, 512
+FLOPS = 2 * (K * H * S + 2 * K2 * H * P + H * N * S)
+
+F32 = mybir.dt.float32
+BF16 = mybir.dt.bfloat16
+I32 = mybir.dt.int32
+U32 = mybir.dt.uint32
+U16 = mybir.dt.uint16
+U8 = mybir.dt.uint8
+FP8X4 = mybir.dt.float8_e4m3fn_x4
+FP4X4 = mybir.dt.float4_e2m1fn_x4
+ALU = mybir.AluOpType
+ACT = mybir.ActivationFunctionType
+
+PART = 128
+PACK = 4
+PASS = PART * PACK
+QUAD = 32
+BANK = 512
+PAGES = 3
+AHEAD = 2
+CHUNKS = (256, 256, 256, 128, 128)
+
+
+def tile_list_crate_freshness_scores_kernel(
+    tc, tab_words, tab_scales, tab2_words, tab2_scales, offs, offs2, pos1, w1_words, w1_scales,
+    cap, w2, w3_words, w3_scales, wgs, gm, w4, out,
+):
+    nc = tc.nc
+    halves = H // PASS
+    slices = [(b, t) for b in range(halves) for t in range(PACK)]
+
+    with ExitStack() as ctx:
+        keep = ctx.enter_context(tc.tile_pool(name="keep", bufs=1))
+        ring = ctx.enter_context(tc.tile_pool(name="ring", bufs=2))
+        shared = ctx.enter_context(tc.tile_pool(name="shared", bufs=1))
+        psum = ctx.enter_context(tc.psum_pool(name="psum", bufs=1))
+
+        def held(name, shape, dtype):
+            return keep.tile(shape, dtype, name=name, align_bytes=64)
+
+        tab2_s = held("tab2_s", [PART, T3], U8)
+        w3_s = held("w3_s", [PART, H], U8)
+        w1_s = held("w1_s", [PART, H], U8)
+        w1_sd1 = held("w1_sd1", [PART, H], U8)
+        tab_s = held("tab_s", [PART, T], U8)
+        v_s1 = held("v_s1", [PART, S], U8)
+        one = held("one", [PART, 1], F32)
+        sin_bias = held("sin_bias", [PART, 1], F32)
+        root2 = held("root2", [PART, 1], F32)
+        nc.vector.memset(one[:], 1.0)
+        nc.vector.tensor_scalar(sin_bias[:], one[:], -math.pi / 8, None, ALU.mult)
+        nc.vector.tensor_scalar(root2[:], one[:], math.sqrt(2.0), None, ALU.mult)
+        pages = [held("page%d" % i, [PART, S], F32) for i in range(PAGES)]
+        for page in pages:
+            nc.vector.memset(page[:], 0.0)
+        for plane in (tab_s, w1_s, v_s1, w1_sd1):
+            nc.vector.memset(plane[:].bitcast(I32), 0)
+
+        def load_plane(queue, plane, rows):
+            for q in range(4):
+                queue.dma_start(
+                    out=plane[QUAD * q : QUAD * (q + 1), :].bitcast(I32),
+                    in_=rows[4 * q : 4 * q + 4, :].bitcast(I32).partition_broadcast(QUAD // 4),
+                )
+
+        idx2 = held("idx2", [PART, P // 16], U16)
+        nc.sync.dma_start(out=idx2[:], in_=offs2)
+        load_plane(nc.sync, tab2_s, tab2_scales[0])
+        tab2_w = held("tab2_w", [PART, T3], U32)
+        nc.sync.dma_start(out=tab2_w[:].bitcast(I32), in_=tab2_words[0].rearrange("p t i -> p (t i)").bitcast(I32))
+        w3_rows = w3_words[0].rearrange("p c i -> p (c i)").bitcast(I32)
+        w3_w = [held("w3_w%d" % b, [PART, PASS], U32) for b in range(halves)]
+        nc.sync.dma_start(out=w3_w[0][:].bitcast(I32), in_=w3_rows[:, 0:PASS])
+        load_plane(nc.sync, w3_s, w3_scales[0])
+        w2_first = [held("w2_first%d" % u, [PART, PACK, PASS // 2], F32) for u in range(2)]
+        for u in range(2):
+            nc.sync.dma_start(out=w2_first[u][:], in_=w2[:, u * PASS // 2 : (u + 1) * PASS // 2].rearrange("(p i) c -> p i c", i=PACK))
+
+        def load_rows(src):
+            raw = ring.tile([PART, PACK, BANK], F32, name="raw", tag="raw")
+            nc.sync.dma_start(out=raw[:], in_=src.rearrange("(p i) c -> p i c", i=PACK))
+            return raw
+
+        places = held("places", [PART, P // 16], U16)
+        nc.sync.dma_start(out=places[:], in_=pos1)
+        wg = shared.tile([PART, PACK, P], F32, name="wg", offset=0)
+        for q in range(4):
+            nc.sync.dma_start(out=wg[QUAD * q : QUAD * (q + 1), :, :], in_=wgs.rearrange("(p t) j -> p t j", t=PACK))
+        nc.sync.dma_start(out=w3_w[1][:].bitcast(I32), in_=w3_rows[:, PASS : 2 * PASS])
+        gm_rows = gm.rearrange("(b p t) j -> b t p j", b=halves, t=PACK)
+        gate = [held("gate%d" % s, [PART, S], F32) for s in range(len(slices))]
+
+        def load_gate(s):
+            b, t = slices[s]
+            nc.sync.dma_start(out=gate[s][:], in_=gm_rows[b, t])
+
+        tab_w = [held("tab_w%d" % a, [PART, T], U32) for a in range(2)]
+
+        def load_tab(a):
+            nc.sync.dma_start(out=tab_w[a][:].bitcast(I32), in_=tab_words[a].rearrange("p t i -> p (t i)").bitcast(I32))
+
+        load_gate(0)
+        w2_second = load_rows(w2[:, PASS : 2 * PASS])
+        load_gate(1)
+        idx = held("idx", [PART, S // 16], U16)
+        nc.sync.dma_start(out=idx[:], in_=offs)
+        caps = held("caps", [PART, halves, PACK], F32)
+        nc.sync.dma_start(out=caps[:], in_=cap.rearrange("(b p t) -> p b t", b=halves, t=PACK))
+        for plane, rows in ((tab_s, tab_scales), (w1_s, w1_scales)):
+            for q in range(4):
+                nc.sync.dma_start(out=plane[QUAD * q : QUAD * q + 8, :].bitcast(I32), in_=rows[:, 4 * q : 4 * q + 4, :].bitcast(I32))
+        load_tab(0)
+        load_gate(2)
+        load_tab(1)
+        load_gate(3)
+        w1_w = held("w1_w", [PART, 2, 2 * H], U8)
+        nc.sync.dma_start(out=w1_w[:].bitcast(I32), in_=w1_words.rearrange("a p c -> p a c").bitcast(I32))
+        load_gate(4)
+        load_gate(5)
+        w4_raw = [load_rows(w4[0:PASS, :])]
+        load_gate(6)
+        w4_raw.append(load_rows(w4[PASS : 2 * PASS, :]))
+        load_gate(7)
+
+        v2_w = held("v2_w", [PART, P], U32)
+        v2_s = held("v2_s", [PART, P], U8)
+        nc.vector.tensor_copy(v2_w[:], tab2_w[:].indirect(idx2[:]))
+        nc.vector.tensor_copy(v2_s[:], tab2_s[:].indirect(idx2[:]))
+        w3_sd = held("w3_sd", [PART, H], U8)
+        nc.vector.tensor_copy(
+            w3_sd[:].rearrange("p (b t q) -> p b t q", b=halves, t=PACK),
+            w3_s[:].rearrange("p (b q t) -> p b t q", b=halves, t=PACK),
+        )
+        w3_wd = []
+        for b in range(halves):
+            wd = held("w3_wd%d" % b, [PART, PASS], U32)
+            nc.scalar.copy(
+                wd[:].rearrange("p (t q) -> p t q", t=PACK),
+                w3_w[b][:].rearrange("p (q t) -> p t q", t=PACK),
+            )
+            w3_wd.append(wd)
+
+        def quantised(name, grouped, width):
+            codes = held(name + "_c", [PART, width], U32)
+            scales = held(name + "_s", [PART, width], U8)
+            nc.vector.quantize_mx(out=codes[:].bitcast(FP8X4), scales=scales[:], in_=grouped)
+            return codes, scales
+
+        def w2_half(b, parts, copy, cuts):
+            grouped = ring.tile([PART, PACK * BANK], BF16, name="grouped", tag="grouped", align_bytes=64)
+            dealt = grouped[:].rearrange("p (t q i) -> p q t i", t=PACK, i=PACK)
+            share = PART // len(parts)
+            for u, raw in enumerate(parts):
+                copy(dealt[:, share * u : share * (u + 1), :, :], raw[:].rearrange("p i (q t) -> p q t i", t=PACK))
+            made = []
+            for t0, t1 in cuts:
+                codes, scales = quantised("w2q%d_%d" % (b, t0), grouped[:, BANK * t0 : BANK * t1], PART * (t1 - t0))
+                for t in range(t1 - t0):
+                    made.append((codes[:, PART * t : PART * (t + 1)], scales[:, PART * t : PART * (t + 1)]))
+            return made
+
+        def weighted(s, w2q):
+            b, t = slices[s]
+            cols = slice(PART * t, PART * (t + 1))
+            arg = psum.tile([PART, P], F32, name="arg", tag="arg", bufs=1)
+            nc.tensor.matmul_mx(
+                out=arg[:], lhsT=w3_wd[b][:, cols].bitcast(FP8X4), lhsT_scale=w3_sd[:, PASS * b + PART * t : PASS * b + PART * (t + 1)],
+                rhs=v2_w[:].bitcast(FP8X4), rhs_scale=v2_s[:], start=True, stop=True,
+            )
+            wave = ring.tile([PART, P], F32, name="wave", tag="wave", bufs=4)
+            nc.scalar.activation(wave[:], arg[:], ACT.Sin, bias=sin_bias[:], scale=0.25)
+            nc.scalar.activation(wave[:], wave[:], ACT.Square)
+            nc.scalar.activation(wave[:], wave[:], ACT.Square, bias=root2[:], scale=-2.0 * math.sqrt(2.0))
+            lin = psum.tile([PART, P], F32, name="lin", tag="lin", bufs=2)
+            nc.tensor.matmul_mx(
+                out=lin[:], lhsT=w2q[t][0].bitcast(FP8X4), lhsT_scale=w2q[t][1],
+                rhs=v2_w[:].bitcast(FP8X4), rhs_scale=v2_s[:], start=True, stop=True,
+            )
+            smell = ring.tile([PART, P], F32, name="smell", tag="smell", bufs=4)
+            nc.vector.scalar_tensor_tensor(smell[:], wave[:], -1.0, lin[:], ALU.add, ALU.add)
+            if s > 0:
+                nc.gpsimd.tensor_tensor(smell[:], smell[:], wg[:, t, :], ALU.mult)
+            return smell
+
+        w2q = [w2_half(0, w2_first, nc.vector.tensor_copy, ((0, 1), (1, 4)))]
+        ready = []
+        for step in range(len(slices) + AHEAD):
+            if step < len(slices):
+                ready.append(weighted(step, w2q[slices[step][0]]))
+            if step == 0:
+                w2q.append(w2_half(1, [w2_second], nc.scalar.copy, ((0, 4),)))
+            s = step - AHEAD
+            if s >= 0:
+                page = pages[s % PAGES]
+                if s == 0:
+                    nc.vector.tensor_tensor(page[:].indirect(places[:]), ready[s][:], wg[:, 0, :], ALU.mult)
+                else:
+                    nc.vector.tensor_copy(page[:].indirect(places[:]), ready[s][:])
+                nc.gpsimd.tensor_tensor(gate[s][:], page[:], gate[s][:], ALU.mult)
+
+        def second_plane(first, second):
+            for q in range(4):
+                nc.sync.dma_start(out=second[QUAD * q : QUAD * q + 4, :].bitcast(I32), in_=first[QUAD * q + 4 : QUAD * q + 8, :].bitcast(I32))
+            return [first, second]
+
+        v_s0 = held("v_s0", [PART, S], U8)
+        nc.vector.tensor_copy(v_s0[:], tab_s[:].indirect(idx[:]))
+        v_s = second_plane(v_s0, v_s1)
+        w1_sd0 = held("w1_sd0", [PART, H], U8)
+        nc.vector.tensor_copy(
+            w1_sd0[:].rearrange("p (b t q) -> p b t q", b=halves, t=PACK),
+            w1_s[:].rearrange("p (b q t) -> p b t q", b=halves, t=PACK),
+        )
+        w1_sd = second_plane(w1_sd0, w1_sd1)
+        v_w = []
+        for a in range(2):
+            vw = held("v_w%d" % a, [PART, S], U32)
+            nc.vector.tensor_copy(vw[:], tab_w[a][:].indirect(idx[:]))
+            v_w.append(vw)
+        w1_wd = []
+        for b in range(halves):
+            wd = held("w1_wd%d" % b, [PART, 2, 2 * PASS], U8)
+            nc.scalar.copy(
+                wd[:].bitcast(U16).rearrange("p a (t q) -> p a t q", t=PACK),
+                w1_w[:, :, 2 * PASS * b : 2 * PASS * (b + 1)].bitcast(U16).rearrange("p a (q t) -> p a t q", t=PACK),
+            )
+            w1_wd.append(wd)
+
+        def make_z(b, c0, width, z):
+            cols = slice(c0, c0 + width)
+            per_bank = BANK // width
+            for t0 in range(0, PACK, per_bank):
+                img = psum.tile([PART, per_bank, width], F32, name="img", tag="img", bufs=3)
+                for u in range(per_bank):
+                    r0 = PART * (t0 + u)
+                    for a in range(2):
+                        nc.tensor.matmul_mx(
+                            out=img[:, u, :], lhsT=w1_wd[b][:, a, 2 * r0 : 2 * (r0 + PART)].bitcast(FP4X4),
+                            lhsT_scale=w1_sd[a][:, PASS * b + r0 : PASS * b + r0 + PART],
+                            rhs=v_w[a][:, cols].bitcast(FP8X4), rhs_scale=v_s[a][:, cols],
+                            start=(a == 0), stop=(a == 1),
+                        )
+                for u in range(per_bank):
+                    t = t0 + u
+                    nc.vector.scalar_tensor_tensor(
+                        z[:, t, :], img[:, u, :], caps[:, b, t : t + 1], gate[PACK * b + t][:, cols], ALU.min, ALU.add
+                    )
+
+        def interleave(copy, zg, z):
+            copy(zg.rearrange("p (c e t) -> p c t e", e=4, t=PACK), z.rearrange("p t (c e) -> p c t e", e=4))
+
+        first_grouped = []
+        for c0 in range(0, S, BANK):
+            z = ring.tile([PART, PACK, BANK], BF16, name="z_first", tag="z_first", bufs=2)
+            make_z(0, c0, BANK, z)
+            zg = ring.tile([PART, PACK * BANK], BF16, name="zg_first", tag="zg_first", bufs=2, align_bytes=64)
+            for u in range(2):
+                interleave(nc.scalar.copy, zg[:, u * 2 * BANK : (u + 1) * 2 * BANK], z[:, :, u * BANK // 2 : (u + 1) * BANK // 2])
+            first_grouped.append(zg)
+        w4q = []
+        for b in range(halves):
+            grouped = ring.tile([PART, PACK * BANK], BF16, name="grouped", tag="grouped", align_bytes=64)
+            for u in range(2):
+                nc.scalar.copy(
+                    grouped[:, u * 2 * BANK : (u + 1) * 2 * BANK].rearrange("p (c e i) -> p c i e", e=4, i=PACK),
+                    w4_raw[b][:, :, u * BANK // 2 : (u + 1) * BANK // 2].rearrange("p i (c e) -> p c i e", e=4),
+                )
+            w4q.append(quantised("w4q%d" % b, grouped[:], N))
+        zq_first = [quantised("zq_first%d" % u, zg[:], BANK) for u, zg in enumerate(first_grouped)]
+
+        out_rows = out.rearrange("(g p) j -> p g j", p=PART)
+
+        def second_z(c0, width):
+            z = shared.tile([PART, PACK, width], BF16, name="z_second%d" % c0, offset=2 * PACK * c0)
+            make_z(1, c0, width, z)
+            zg = ring.tile([PART, PACK * width], BF16, name="zg", tag="zg", bufs=3, align_bytes=64)
+            interleave(nc.scalar.copy, zg[:], z[:])
+            return zg
+
+        def finish(c0, width, zg):
+            codes, scales = zq_first[c0 // BANK]
+            inner = slice(c0 % BANK, c0 % BANK + width)
+            second = quantised("zq_second%d" % c0, zg[:], width)
+            zq = [(codes[:, inner], scales[:, inner]), (second[0][:], second[1][:])]
+            per_bank = BANK // width
+            staged = ring.tile([PART, N // PART, width], F32, name="staged", tag="staged", bufs=3)
+            for g0 in range(0, N // PART, per_bank):
+                acc = psum.tile([PART, per_bank, width], F32, name="acc", tag="acc", bufs=2)
+                for u in range(per_bank):
+                    rows = slice(PART * (g0 + u), PART * (g0 + u + 1))
+                    for b in range(halves):
+                        nc.tensor.matmul_mx(
+                            out=acc[:, u, :], lhsT=w4q[b][0][:, rows].bitcast(FP8X4), lhsT_scale=w4q[b][1][:, rows],
+                            rhs=zq[b][0].bitcast(FP8X4), rhs_scale=zq[b][1],
+                            start=(b == 0), stop=(b == halves - 1),
+                        )
+                nc.scalar.copy(staged[:, g0 : g0 + per_bank, :], acc[:])
+            nc.sync.dma_start(out=out_rows[:, :, c0 : c0 + width], in_=staged[:])
+
+        starts = [sum(CHUNKS[:i]) for i in range(len(CHUNKS))]
+        waiting = None
+        for c0, width in zip(starts, CHUNKS):
+            zg = second_z(c0, width)
+            if waiting is not None:
+                finish(*waiting)
+            waiting = (c0, width, zg)
+        finish(*waiting)

@@ -24,6 +24,9 @@ QUAD = 32
 BANK = 512
 PAGES = 3
 AHEAD = 2
+SMELLS = 4
+SMELL_AT = 4 * PACK * P
+LATE_AT = SMELL_AT + 4 * P * (SMELLS - 1)
 CHUNKS = (256, 256, 256, 128, 128)
 
 
@@ -116,17 +119,27 @@ def tile_list_crate_freshness_scores_kernel(
             for q in range(4):
                 nc.sync.dma_start(out=plane[QUAD * q : QUAD * q + 8, :].bitcast(I32), in_=rows[:, 4 * q : 4 * q + 4, :].bitcast(I32))
         load_tab(0)
-        load_gate(2)
         load_tab(1)
-        load_gate(3)
         w1_w = held("w1_w", [PART, 2, 2 * H], U8)
         nc.sync.dma_start(out=w1_w[:].bitcast(I32), in_=w1_words.rearrange("a p c -> p a c").bitcast(I32))
-        load_gate(4)
-        load_gate(5)
-        w4_raw = [load_rows(w4[0:PASS, :])]
-        load_gate(6)
-        w4_raw.append(load_rows(w4[PASS : 2 * PASS, :]))
-        load_gate(7)
+        def second_plane(first, second):
+            for q in range(4):
+                nc.sync.dma_start(out=second[QUAD * q : QUAD * q + 4, :].bitcast(I32), in_=first[QUAD * q + 4 : QUAD * q + 8, :].bitcast(I32))
+            return [first, second]
+
+        v_s0 = held("v_s0", [PART, S], U8)
+        nc.vector.tensor_copy(v_s0[:], tab_s[:].indirect(idx[:]))
+        v_s = second_plane(v_s0, v_s1)
+        w1_sd0 = held("w1_sd0", [PART, H], U8)
+        nc.gpsimd.tensor_copy(
+            w1_sd0[:].rearrange("p (b t q) -> p b t q", b=halves, t=PACK),
+            w1_s[:].rearrange("p (b q t) -> p b t q", b=halves, t=PACK),
+        )
+        w1_sd = second_plane(w1_sd0, w1_sd1)
+        load_gate(2)
+        w4_raw = [load_rows(w4[PASS * b : PASS * (b + 1), :]) for b in range(halves)]
+        for s in range(3, len(slices)):
+            load_gate(s)
 
         v2_w = held("v2_w", [PART, P], U32)
         v2_s = held("v2_s", [PART, P], U8)
@@ -146,9 +159,10 @@ def tile_list_crate_freshness_scores_kernel(
             )
             w3_wd.append(wd)
 
-        def quantised(name, grouped, width):
+        def quantised(name, grouped, width, scales=None):
             codes = held(name + "_c", [PART, width], U32)
-            scales = held(name + "_s", [PART, width], U8)
+            if scales is None:
+                scales = held(name + "_s", [PART, width], U8)
             nc.vector.quantize_mx(out=codes[:].bitcast(FP8X4), scales=scales[:], in_=grouped)
             return codes, scales
 
@@ -182,7 +196,7 @@ def tile_list_crate_freshness_scores_kernel(
                 out=lin[:], lhsT=w2q[t][0].bitcast(FP8X4), lhsT_scale=w2q[t][1],
                 rhs=v2_w[:].bitcast(FP8X4), rhs_scale=v2_s[:], start=True, stop=True,
             )
-            smell = ring.tile([PART, P], F32, name="smell", tag="smell", bufs=4)
+            smell = shared.tile([PART, P], F32, name="smell%d" % s, offset=SMELL_AT + 4 * P * (s % SMELLS))
             nc.vector.scalar_tensor_tensor(smell[:], wave[:], -1.0, lin[:], ALU.add, ALU.add)
             if s > 0:
                 nc.gpsimd.tensor_tensor(smell[:], smell[:], wg[:, t, :], ALU.mult)
@@ -202,22 +216,9 @@ def tile_list_crate_freshness_scores_kernel(
                     nc.vector.tensor_tensor(page[:].indirect(places[:]), ready[s][:], wg[:, 0, :], ALU.mult)
                 else:
                     nc.vector.tensor_copy(page[:].indirect(places[:]), ready[s][:])
-                nc.gpsimd.tensor_tensor(gate[s][:], page[:], gate[s][:], ALU.mult)
+                if s < len(slices) - 1:
+                    nc.gpsimd.tensor_tensor(gate[s][:], page[:], gate[s][:], ALU.mult)
 
-        def second_plane(first, second):
-            for q in range(4):
-                nc.sync.dma_start(out=second[QUAD * q : QUAD * q + 4, :].bitcast(I32), in_=first[QUAD * q + 4 : QUAD * q + 8, :].bitcast(I32))
-            return [first, second]
-
-        v_s0 = held("v_s0", [PART, S], U8)
-        nc.vector.tensor_copy(v_s0[:], tab_s[:].indirect(idx[:]))
-        v_s = second_plane(v_s0, v_s1)
-        w1_sd0 = held("w1_sd0", [PART, H], U8)
-        nc.vector.tensor_copy(
-            w1_sd0[:].rearrange("p (b t q) -> p b t q", b=halves, t=PACK),
-            w1_s[:].rearrange("p (b q t) -> p b t q", b=halves, t=PACK),
-        )
-        w1_sd = second_plane(w1_sd0, w1_sd1)
         v_w = []
         for a in range(2):
             vw = held("v_w%d" % a, [PART, S], U32)
@@ -263,7 +264,7 @@ def tile_list_crate_freshness_scores_kernel(
             for u in range(2):
                 interleave(nc.scalar.copy, zg[:, u * 2 * BANK : (u + 1) * 2 * BANK], z[:, :, u * BANK // 2 : (u + 1) * BANK // 2])
             first_grouped.append(zg)
-        w4q = []
+        w4_grouped = []
         for b in range(halves):
             grouped = ring.tile([PART, PACK * BANK], BF16, name="grouped", tag="grouped", align_bytes=64)
             for u in range(2):
@@ -271,19 +272,28 @@ def tile_list_crate_freshness_scores_kernel(
                     grouped[:, u * 2 * BANK : (u + 1) * 2 * BANK].rearrange("p (c e i) -> p c i e", e=4, i=PACK),
                     w4_raw[b][:, :, u * BANK // 2 : (u + 1) * BANK // 2].rearrange("p i (c e) -> p c i e", e=4),
                 )
-            w4q.append(quantised("w4q%d" % b, grouped[:], N))
-        zq_first = [quantised("zq_first%d" % u, zg[:], BANK) for u, zg in enumerate(first_grouped)]
+            w4_grouped.append(grouped)
+        late = [shared.tile([PART, BANK], U8, name="late%d" % u, offset=LATE_AT + BANK * u, align_bytes=64) for u in range(4)]
+        w4q = []
+        zq_first = []
 
         out_rows = out.rearrange("(g p) j -> p g j", p=PART)
 
         def second_z(c0, width):
             z = shared.tile([PART, PACK, width], BF16, name="z_second%d" % c0, offset=2 * PACK * c0)
+            last = gate[-1][:, c0 : c0 + width]
+            nc.vector.tensor_tensor(last, pages[(len(slices) - 1) % PAGES][:, c0 : c0 + width], last, ALU.mult)
             make_z(1, c0, width, z)
             zg = ring.tile([PART, PACK * width], BF16, name="zg", tag="zg", bufs=3, align_bytes=64)
             interleave(nc.scalar.copy, zg[:], z[:])
             return zg
 
         def finish(c0, width, zg):
+            if c0 == 0:
+                w4q.extend(quantised("w4q%d" % b, w4_grouped[b][:], N, late[b]) for b in range(halves))
+            if c0 % BANK == 0:
+                u = c0 // BANK
+                zq_first.append(quantised("zq_first%d" % u, first_grouped[u][:], BANK, late[halves + u]))
             codes, scales = zq_first[c0 // BANK]
             inner = slice(c0 % BANK, c0 % BANK + width)
             second = quantised("zq_second%d" % c0, zg[:], width)

@@ -2,6 +2,7 @@ import math
 from contextlib import ExitStack
 
 import concourse.mybir as mybir
+from concourse.masks import make_identity
 
 K, K2, H, N, T, S, T3, P = 1024, 512, 1024, 512, 4096, 1024, 2048, 512
 FLOPS = 2 * (K * H * S + 2 * K2 * H * P + H * N * S)
@@ -23,10 +24,8 @@ PASS = PART * PACK
 QUAD = 32
 BANK = 512
 PAGES = 3
-AHEAD = 2
-SMELLS = 4
+TURN_FROM = 2
 SMELL_AT = 4 * PACK * P
-LATE_AT = SMELL_AT + 4 * P * (SMELLS - 1)
 CHUNKS = (256, 256, 256, 128, 128)
 
 
@@ -59,10 +58,12 @@ def tile_list_crate_freshness_scores_kernel(
         nc.vector.memset(one[:], 1.0)
         nc.vector.tensor_scalar(sin_bias[:], one[:], -math.pi / 8, None, ALU.mult)
         nc.vector.tensor_scalar(root2[:], one[:], math.sqrt(2.0), None, ALU.mult)
+        ident = held("ident", [PART, PART], F32)
+        make_identity(nc, ident[:])
         pages = [held("page%d" % i, [PART, S], F32) for i in range(PAGES)]
         for page in pages:
             nc.vector.memset(page[:], 0.0)
-        for plane in (tab_s, w1_s, v_s1, w1_sd1):
+        for plane in (w1_s, tab_s, v_s1, w1_sd1):
             nc.vector.memset(plane[:].bitcast(I32), 0)
 
         def load_plane(queue, plane, rows):
@@ -81,7 +82,9 @@ def tile_list_crate_freshness_scores_kernel(
         w3_w = [held("w3_w%d" % b, [PART, PASS], U32) for b in range(halves)]
         nc.sync.dma_start(out=w3_w[0][:].bitcast(I32), in_=w3_rows[:, 0:PASS])
         load_plane(nc.sync, w3_s, w3_scales[0])
-        w2_first = [held("w2_first%d" % u, [PART, PACK, PASS // 2], F32) for u in range(2)]
+        w2_first = [
+            shared.tile([PART, PACK, PASS // 2], F32, name="w2_first%d" % u, offset=SMELL_AT + 4 * P * (PACK + 2 * u)) for u in range(2)
+        ]
         for u in range(2):
             nc.sync.dma_start(out=w2_first[u][:], in_=w2[:, u * PASS // 2 : (u + 1) * PASS // 2].rearrange("(p i) c -> p i c", i=PACK))
 
@@ -90,12 +93,15 @@ def tile_list_crate_freshness_scores_kernel(
             nc.sync.dma_start(out=raw[:], in_=src.rearrange("(p i) c -> p i c", i=PACK))
             return raw
 
+        def load_two_planes(plane, rows):
+            for q in range(4):
+                nc.sync.dma_start(out=plane[QUAD * q : QUAD * q + 8, :].bitcast(I32), in_=rows[:, 4 * q : 4 * q + 4, :].bitcast(I32))
+
         places = held("places", [PART, P // 16], U16)
         nc.sync.dma_start(out=places[:], in_=pos1)
         wg = shared.tile([PART, PACK, P], F32, name="wg", offset=0)
         for q in range(4):
             nc.sync.dma_start(out=wg[QUAD * q : QUAD * (q + 1), :, :], in_=wgs.rearrange("(p t) j -> p t j", t=PACK))
-        nc.sync.dma_start(out=w3_w[1][:].bitcast(I32), in_=w3_rows[:, PASS : 2 * PASS])
         gm_rows = gm.rearrange("(b p t) j -> b t p j", b=halves, t=PACK)
         gate = [held("gate%d" % s, [PART, S], F32) for s in range(len(slices))]
 
@@ -109,60 +115,44 @@ def tile_list_crate_freshness_scores_kernel(
             nc.sync.dma_start(out=tab_w[a][:].bitcast(I32), in_=tab_words[a].rearrange("p t i -> p (t i)").bitcast(I32))
 
         load_gate(0)
+        nc.sync.dma_start(out=w3_w[1][:].bitcast(I32), in_=w3_rows[:, PASS : 2 * PASS])
         w2_second = load_rows(w2[:, PASS : 2 * PASS])
         load_gate(1)
         idx = held("idx", [PART, S // 16], U16)
         nc.sync.dma_start(out=idx[:], in_=offs)
         caps = held("caps", [PART, halves, PACK], F32)
         nc.sync.dma_start(out=caps[:], in_=cap.rearrange("(b p t) -> p b t", b=halves, t=PACK))
-        for plane, rows in ((tab_s, tab_scales), (w1_s, w1_scales)):
-            for q in range(4):
-                nc.sync.dma_start(out=plane[QUAD * q : QUAD * q + 8, :].bitcast(I32), in_=rows[:, 4 * q : 4 * q + 4, :].bitcast(I32))
+        load_two_planes(tab_s, tab_scales)
+        load_two_planes(w1_s, w1_scales)
         load_tab(0)
         load_tab(1)
         w1_w = held("w1_w", [PART, 2, 2 * H], U8)
         nc.sync.dma_start(out=w1_w[:].bitcast(I32), in_=w1_words.rearrange("a p c -> p a c").bitcast(I32))
-        def second_plane(first, second):
-            for q in range(4):
-                nc.sync.dma_start(out=second[QUAD * q : QUAD * q + 4, :].bitcast(I32), in_=first[QUAD * q + 4 : QUAD * q + 8, :].bitcast(I32))
-            return [first, second]
-
-        v_s0 = held("v_s0", [PART, S], U8)
-        nc.vector.tensor_copy(v_s0[:], tab_s[:].indirect(idx[:]))
-        v_s = second_plane(v_s0, v_s1)
-        w1_sd0 = held("w1_sd0", [PART, H], U8)
-        nc.gpsimd.tensor_copy(
-            w1_sd0[:].rearrange("p (b t q) -> p b t q", b=halves, t=PACK),
-            w1_s[:].rearrange("p (b q t) -> p b t q", b=halves, t=PACK),
-        )
-        w1_sd = second_plane(w1_sd0, w1_sd1)
         load_gate(2)
+        load_gate(3)
         w4_raw = [load_rows(w4[PASS * b : PASS * (b + 1), :]) for b in range(halves)]
-        for s in range(3, len(slices)):
+        for s in range(4, len(slices)):
             load_gate(s)
 
         v2_w = held("v2_w", [PART, P], U32)
         v2_s = held("v2_s", [PART, P], U8)
-        nc.vector.tensor_copy(v2_w[:], tab2_w[:].indirect(idx2[:]))
         nc.vector.tensor_copy(v2_s[:], tab2_s[:].indirect(idx2[:]))
+        nc.vector.tensor_copy(v2_w[:], tab2_w[:].indirect(idx2[:]))
         w3_sd = held("w3_sd", [PART, H], U8)
-        nc.vector.tensor_copy(
-            w3_sd[:].rearrange("p (b t q) -> p b t q", b=halves, t=PACK),
-            w3_s[:].rearrange("p (b q t) -> p b t q", b=halves, t=PACK),
-        )
-        w3_wd = []
-        for b in range(halves):
-            wd = held("w3_wd%d" % b, [PART, PASS], U32)
-            nc.scalar.copy(
-                wd[:].rearrange("p (t q) -> p t q", t=PACK),
-                w3_w[b][:].rearrange("p (q t) -> p t q", t=PACK),
-            )
-            w3_wd.append(wd)
+        w3_sd_view = w3_sd[:].rearrange("p (b t q) -> p b t q", b=halves, t=PACK)
+        w3_s_view = w3_s[:].rearrange("p (b q t) -> p b t q", b=halves, t=PACK)
+        nc.vector.tensor_copy(w3_sd_view[:, 0, 0, :], w3_s_view[:, 0, 0, :])
 
-        def quantised(name, grouped, width, scales=None):
+        def deal_w3(b):
+            wd = held("w3_wd%d" % b, [PART, PASS], U32)
+            nc.scalar.copy(wd[:].rearrange("p (t q) -> p t q", t=PACK), w3_w[b][:].rearrange("p (q t) -> p t q", t=PACK))
+            return wd
+
+        w3_wd = [deal_w3(0)]
+
+        def quantised(name, grouped, width):
             codes = held(name + "_c", [PART, width], U32)
-            if scales is None:
-                scales = held(name + "_s", [PART, width], U8)
+            scales = held(name + "_s", [PART, width], U8)
             nc.vector.quantize_mx(out=codes[:].bitcast(FP8X4), scales=scales[:], in_=grouped)
             return codes, scales
 
@@ -179,65 +169,114 @@ def tile_list_crate_freshness_scores_kernel(
                     made.append((codes[:, PART * t : PART * (t + 1)], scales[:, PART * t : PART * (t + 1)]))
             return made
 
-        def weighted(s, w2q):
-            b, t = slices[s]
-            cols = slice(PART * t, PART * (t + 1))
-            arg = psum.tile([PART, P], F32, name="arg", tag="arg", bufs=1)
-            nc.tensor.matmul_mx(
-                out=arg[:], lhsT=w3_wd[b][:, cols].bitcast(FP8X4), lhsT_scale=w3_sd[:, PASS * b + PART * t : PASS * b + PART * (t + 1)],
-                rhs=v2_w[:].bitcast(FP8X4), rhs_scale=v2_s[:], start=True, stop=True,
-            )
-            wave = ring.tile([PART, P], F32, name="wave", tag="wave", bufs=4)
-            nc.scalar.activation(wave[:], arg[:], ACT.Sin, bias=sin_bias[:], scale=0.25)
+        def sine_plus_one(arg, turned):
+            wave = ring.tile([PART, P], F32, name="wave", tag="wave" if turned else "wave_first", bufs=2 if turned else 1)
+            nc.scalar.activation(wave[:], arg, ACT.Sin, bias=sin_bias[:], scale=0.25)
             nc.scalar.activation(wave[:], wave[:], ACT.Square)
             nc.scalar.activation(wave[:], wave[:], ACT.Square, bias=root2[:], scale=-2.0 * math.sqrt(2.0))
-            lin = psum.tile([PART, P], F32, name="lin", tag="lin", bufs=2)
-            nc.tensor.matmul_mx(
-                out=lin[:], lhsT=w2q[t][0].bitcast(FP8X4), lhsT_scale=w2q[t][1],
-                rhs=v2_w[:].bitcast(FP8X4), rhs_scale=v2_s[:], start=True, stop=True,
-            )
-            smell = shared.tile([PART, P], F32, name="smell%d" % s, offset=SMELL_AT + 4 * P * (s % SMELLS))
-            nc.vector.scalar_tensor_tensor(smell[:], wave[:], -1.0, lin[:], ALU.add, ALU.add)
-            if s > 0:
-                nc.gpsimd.tensor_tensor(smell[:], smell[:], wg[:, t, :], ALU.mult)
+            return wave
+
+        def product(tag, weight, turned):
+            bank = psum.tile([PART, P], F32, name=tag, tag=tag, bufs=1)
+            codes, scales = weight
+            if turned:
+                for j0 in range(0, P, PART):
+                    cols = slice(j0, j0 + PART)
+                    nc.tensor.matmul_mx(
+                        out=bank[:, cols], lhsT=v2_w[:, cols].bitcast(FP8X4), lhsT_scale=v2_s[:, cols],
+                        rhs=codes.bitcast(FP8X4), rhs_scale=scales, start=True, stop=True,
+                    )
+            else:
+                nc.tensor.matmul_mx(
+                    out=bank[:], lhsT=codes.bitcast(FP8X4), lhsT_scale=scales,
+                    rhs=v2_w[:].bitcast(FP8X4), rhs_scale=v2_s[:], start=True, stop=True,
+                )
+            return bank
+
+        def smell_of(s, w2q):
+            b, t = slices[s]
+            turned = s >= TURN_FROM
+            w3_part = (w3_wd[b][:, PART * t : PART * (t + 1)], w3_sd[:, PART * s : PART * (s + 1)])
+            wave = sine_plus_one(product("arg", w3_part, turned)[:], turned)
+            lin = product("lin", w2q[t], turned)
+            smell = shared.tile([PART, P], F32, name="smell%d" % s, offset=SMELL_AT + 4 * P * s)
+            if not turned:
+                nc.vector.scalar_tensor_tensor(smell[:], wave[:], -1.0, lin[:], ALU.add, ALU.add)
+                return smell
+            lin_out = ring.tile([PART, P], F32, name="lin_out", tag="lin_out", bufs=2)
+            nc.scalar.copy(lin_out[:], lin[:])
+            total = psum.tile([PART, P], F32, name="total", tag="total", bufs=1)
+            for j0 in range(0, P, PART):
+                cols = slice(j0, j0 + PART)
+                nc.tensor.matmul(total[:, cols], lhsT=lin_out[:, cols], rhs=ident[:], is_transpose=True, start=True, stop=False)
+                nc.tensor.matmul(total[:, cols], lhsT=wave[:, cols], rhs=ident[:], is_transpose=True, start=False, stop=True)
+            nc.scalar.activation(smell[:], total[:], ACT.Copy, bias=-1.0)
             return smell
 
-        w2q = [w2_half(0, w2_first, nc.vector.tensor_copy, ((0, 1), (1, 4)))]
-        ready = []
-        for step in range(len(slices) + AHEAD):
-            if step < len(slices):
-                ready.append(weighted(step, w2q[slices[step][0]]))
-            if step == 0:
-                w2q.append(w2_half(1, [w2_second], nc.scalar.copy, ((0, 4),)))
-            s = step - AHEAD
-            if s >= 0:
-                page = pages[s % PAGES]
-                if s == 0:
-                    nc.vector.tensor_tensor(page[:].indirect(places[:]), ready[s][:], wg[:, 0, :], ALU.mult)
-                else:
-                    nc.vector.tensor_copy(page[:].indirect(places[:]), ready[s][:])
-                if s < len(slices) - 1:
-                    nc.gpsimd.tensor_tensor(gate[s][:], page[:], gate[s][:], ALU.mult)
-
-        v_w = []
-        for a in range(2):
-            vw = held("v_w%d" % a, [PART, S], U32)
-            nc.vector.tensor_copy(vw[:], tab_w[a][:].indirect(idx[:]))
-            v_w.append(vw)
-        w1_wd = []
-        for b in range(halves):
+        def deal_w1(b):
             wd = held("w1_wd%d" % b, [PART, 2, 2 * PASS], U8)
             nc.scalar.copy(
                 wd[:].bitcast(U16).rearrange("p a (t q) -> p a t q", t=PACK),
                 w1_w[:, :, 2 * PASS * b : 2 * PASS * (b + 1)].bitcast(U16).rearrange("p a (q t) -> p a t q", t=PACK),
             )
-            w1_wd.append(wd)
+            return wd
 
-        def make_z(b, c0, width, z):
+        w2q = [w2_half(0, w2_first, nc.vector.tensor_copy, ((0, 1), (1, 4)))]
+        nc.vector.tensor_copy(w3_sd_view[:, 0, 1:, :], w3_s_view[:, 0, 1:, :])
+        nc.vector.tensor_copy(w3_sd_view[:, 1, :, :], w3_s_view[:, 1, :, :])
+        for s, (b, t) in enumerate(slices):
+            if s == 3:
+                w3_wd.append(deal_w3(1))
+                w2q.append(w2_half(1, [w2_second], nc.scalar.copy, ((0, 4),)))
+            smell = smell_of(s, w2q[b])
+            page = pages[s % PAGES]
+            nc.vector.tensor_tensor(page[:].indirect(places[:]), smell[:], wg[:, t, :], ALU.mult)
+            if s < len(slices) - 1:
+                nc.vector.tensor_tensor(gate[s][:], page[:], gate[s][:], ALU.mult)
+        w1_wd = [deal_w1(b) for b in range(halves)]
+
+        def second_plane(first, second):
+            for q in range(4):
+                nc.sync.dma_start(out=second[QUAD * q : QUAD * q + 4, :].bitcast(I32), in_=first[QUAD * q + 4 : QUAD * q + 8, :].bitcast(I32))
+            return [first, second]
+
+        v_s0 = held("v_s0", [PART, S], U8)
+        nc.vector.tensor_copy(v_s0[:], tab_s[:].indirect(idx[:]))
+        v_s = second_plane(v_s0, v_s1)
+        w1_sd0 = held("w1_sd0", [PART, H], U8)
+        nc.vector.tensor_copy(
+            w1_sd0[:].rearrange("p (b t q) -> p b t q", b=halves, t=PACK),
+            w1_s[:].rearrange("p (b q t) -> p b t q", b=halves, t=PACK),
+        )
+        w1_sd = second_plane(w1_sd0, w1_sd1)
+        v_w = []
+        for a in range(2):
+            vw = held("v_w%d" % a, [PART, S], U32)
+            nc.vector.tensor_copy(vw[:], tab_w[a][:].indirect(idx[:]))
+            v_w.append(vw)
+        w4q = []
+        for b in range(halves):
+            grouped = ring.tile([PART, PACK * BANK], BF16, name="grouped", tag="grouped", align_bytes=64)
+            for u in range(2):
+                nc.scalar.copy(
+                    grouped[:, u * 2 * BANK : (u + 1) * 2 * BANK].rearrange("p (c e i) -> p c i e", e=4, i=PACK),
+                    w4_raw[b][:, :, u * BANK // 2 : (u + 1) * BANK // 2].rearrange("p i (c e) -> p c i e", e=4),
+                )
+            w4q.append(quantised("w4q%d" % b, grouped[:], N))
+
+        out_rows = out.rearrange("(g p) j -> p g j", p=PART)
+        img_banks = ["arg", "lin", "total", "img0", "img1", "img2"]
+
+        def make_z(b, c0, width, copy):
             cols = slice(c0, c0 + width)
             per_bank = BANK // width
+            if b == halves - 1 and c0 == 0:
+                nc.vector.tensor_tensor(gate[-1][:], pages[(len(slices) - 1) % PAGES][:], gate[-1][:], ALU.mult)
+            z = ring.tile([PART, PACK, width], BF16, name="z", tag="z", bufs=4)
             for t0 in range(0, PACK, per_bank):
-                img = psum.tile([PART, per_bank, width], F32, name="img", tag="img", bufs=3)
+                tag = img_banks.pop(0)
+                img_banks.append(tag)
+                img = psum.tile([PART, per_bank, width], F32, name="img", tag=tag, bufs=1)
                 for u in range(per_bank):
                     r0 = PART * (t0 + u)
                     for a in range(2):
@@ -252,52 +291,12 @@ def tile_list_crate_freshness_scores_kernel(
                     nc.vector.scalar_tensor_tensor(
                         z[:, t, :], img[:, u, :], caps[:, b, t : t + 1], gate[PACK * b + t][:, cols], ALU.min, ALU.add
                     )
-
-        def interleave(copy, zg, z):
-            copy(zg.rearrange("p (c e t) -> p c t e", e=4, t=PACK), z.rearrange("p t (c e) -> p c t e", e=4))
-
-        first_grouped = []
-        for c0 in range(0, S, BANK):
-            z = ring.tile([PART, PACK, BANK], BF16, name="z_first", tag="z_first", bufs=2)
-            make_z(0, c0, BANK, z)
-            zg = ring.tile([PART, PACK * BANK], BF16, name="zg_first", tag="zg_first", bufs=2, align_bytes=64)
-            for u in range(2):
-                interleave(nc.scalar.copy, zg[:, u * 2 * BANK : (u + 1) * 2 * BANK], z[:, :, u * BANK // 2 : (u + 1) * BANK // 2])
-            first_grouped.append(zg)
-        w4_grouped = []
-        for b in range(halves):
-            grouped = ring.tile([PART, PACK * BANK], BF16, name="grouped", tag="grouped", align_bytes=64)
-            for u in range(2):
-                nc.scalar.copy(
-                    grouped[:, u * 2 * BANK : (u + 1) * 2 * BANK].rearrange("p (c e i) -> p c i e", e=4, i=PACK),
-                    w4_raw[b][:, :, u * BANK // 2 : (u + 1) * BANK // 2].rearrange("p i (c e) -> p c i e", e=4),
-                )
-            w4_grouped.append(grouped)
-        late = [shared.tile([PART, BANK], U8, name="late%d" % u, offset=LATE_AT + BANK * u, align_bytes=64) for u in range(4)]
-        w4q = []
-        zq_first = []
-
-        out_rows = out.rearrange("(g p) j -> p g j", p=PART)
-
-        def second_z(c0, width):
-            z = shared.tile([PART, PACK, width], BF16, name="z_second%d" % c0, offset=2 * PACK * c0)
-            last = gate[-1][:, c0 : c0 + width]
-            nc.vector.tensor_tensor(last, pages[(len(slices) - 1) % PAGES][:, c0 : c0 + width], last, ALU.mult)
-            make_z(1, c0, width, z)
-            zg = ring.tile([PART, PACK * width], BF16, name="zg", tag="zg", bufs=3, align_bytes=64)
-            interleave(nc.scalar.copy, zg[:], z[:])
+            zg = ring.tile([PART, PACK * width], BF16, name="zg", tag="zg", bufs=4, align_bytes=64)
+            copy(zg[:].rearrange("p (c e t) -> p c t e", e=4, t=PACK), z[:].rearrange("p t (c e) -> p c t e", e=4))
             return zg
 
-        def finish(c0, width, zg):
-            if c0 == 0:
-                w4q.extend(quantised("w4q%d" % b, w4_grouped[b][:], N, late[b]) for b in range(halves))
-            if c0 % BANK == 0:
-                u = c0 // BANK
-                zq_first.append(quantised("zq_first%d" % u, first_grouped[u][:], BANK, late[halves + u]))
-            codes, scales = zq_first[c0 // BANK]
-            inner = slice(c0 % BANK, c0 % BANK + width)
-            second = quantised("zq_second%d" % c0, zg[:], width)
-            zq = [(codes[:, inner], scales[:, inner]), (second[0][:], second[1][:])]
+        def finish(c0, width, grouped):
+            zq = [quantised("zq%d_%d" % (c0, b), grouped[b][:], width) for b in range(halves)]
             per_bank = BANK // width
             staged = ring.tile([PART, N // PART, width], F32, name="staged", tag="staged", bufs=3)
             for g0 in range(0, N // PART, per_bank):
@@ -307,7 +306,7 @@ def tile_list_crate_freshness_scores_kernel(
                     for b in range(halves):
                         nc.tensor.matmul_mx(
                             out=acc[:, u, :], lhsT=w4q[b][0][:, rows].bitcast(FP8X4), lhsT_scale=w4q[b][1][:, rows],
-                            rhs=zq[b][0].bitcast(FP8X4), rhs_scale=zq[b][1],
+                            rhs=zq[b][0][:].bitcast(FP8X4), rhs_scale=zq[b][1][:],
                             start=(b == 0), stop=(b == halves - 1),
                         )
                 nc.scalar.copy(staged[:, g0 : g0 + per_bank, :], acc[:])
@@ -316,8 +315,9 @@ def tile_list_crate_freshness_scores_kernel(
         starts = [sum(CHUNKS[:i]) for i in range(len(CHUNKS))]
         waiting = None
         for c0, width in zip(starts, CHUNKS):
-            zg = second_z(c0, width)
+            final = c0 == starts[-1]
+            grouped = [make_z(b, c0, width, nc.vector.tensor_copy if final and b == halves - 1 else nc.scalar.copy) for b in range(halves)]
             if waiting is not None:
                 finish(*waiting)
-            waiting = (c0, width, zg)
+            waiting = (c0, width, grouped)
         finish(*waiting)

@@ -24,8 +24,9 @@ PASS = PART * PACK
 QUAD = 32
 BANK = 512
 PAGES = 3
-TURN_FROM = 2
-SMELL_AT = 4 * PACK * P
+AHEAD = 2
+FIRST_AT = 4 * PACK * P
+SECOND_AT = 2 * FIRST_AT
 CHUNKS = (256, 256, 256, 128, 128)
 
 
@@ -57,13 +58,14 @@ def tile_list_crate_freshness_scores_kernel(
         root2 = held("root2", [PART, 1], F32)
         nc.vector.memset(one[:], 1.0)
         nc.vector.tensor_scalar(sin_bias[:], one[:], -math.pi / 8, None, ALU.mult)
-        nc.vector.tensor_scalar(root2[:], one[:], math.sqrt(2.0), None, ALU.mult)
+        nc.scalar.activation(root2[:], one[:], ACT.Sin, scale=math.pi / 4)
+        nc.vector.tensor_scalar(root2[:], root2[:], 2.0, None, ALU.mult)
         ident = held("ident", [PART, PART], F32)
         make_identity(nc, ident[:])
         pages = [held("page%d" % i, [PART, S], F32) for i in range(PAGES)]
         for page in pages:
             nc.vector.memset(page[:], 0.0)
-        for plane in (w1_s, tab_s, v_s1, w1_sd1):
+        for plane in (tab_s, w1_s, v_s1, w1_sd1):
             nc.vector.memset(plane[:].bitcast(I32), 0)
 
         def load_plane(queue, plane, rows):
@@ -83,7 +85,7 @@ def tile_list_crate_freshness_scores_kernel(
         nc.sync.dma_start(out=w3_w[0][:].bitcast(I32), in_=w3_rows[:, 0:PASS])
         load_plane(nc.sync, w3_s, w3_scales[0])
         w2_first = [
-            shared.tile([PART, PACK, PASS // 2], F32, name="w2_first%d" % u, offset=SMELL_AT + 4 * P * (PACK + 2 * u)) for u in range(2)
+            shared.tile([PART, PACK, PASS // 2], F32, name="w2_first%d" % u, offset=SECOND_AT + u * FIRST_AT // 2) for u in range(2)
         ]
         for u in range(2):
             nc.sync.dma_start(out=w2_first[u][:], in_=w2[:, u * PASS // 2 : (u + 1) * PASS // 2].rearrange("(p i) c -> p i c", i=PACK))
@@ -114,25 +116,39 @@ def tile_list_crate_freshness_scores_kernel(
         def load_tab(a):
             nc.sync.dma_start(out=tab_w[a][:].bitcast(I32), in_=tab_words[a].rearrange("p t i -> p (t i)").bitcast(I32))
 
-        load_gate(0)
-        nc.sync.dma_start(out=w3_w[1][:].bitcast(I32), in_=w3_rows[:, PASS : 2 * PASS])
-        w2_second = load_rows(w2[:, PASS : 2 * PASS])
-        load_gate(1)
         idx = held("idx", [PART, S // 16], U16)
         nc.sync.dma_start(out=idx[:], in_=offs)
+        load_two_planes(tab_s, tab_scales)
+        w2_second = load_rows(w2[:, PASS : 2 * PASS])
+        nc.sync.dma_start(out=w3_w[1][:].bitcast(I32), in_=w3_rows[:, PASS : 2 * PASS])
         caps = held("caps", [PART, halves, PACK], F32)
         nc.sync.dma_start(out=caps[:], in_=cap.rearrange("(b p t) -> p b t", b=halves, t=PACK))
-        load_two_planes(tab_s, tab_scales)
-        load_two_planes(w1_s, w1_scales)
+        for s in range(4):
+            if s == 3:
+                load_two_planes(w1_s, w1_scales)
+            load_gate(s)
         load_tab(0)
+        for s in range(4, len(slices)):
+            load_gate(s)
         load_tab(1)
         w1_w = held("w1_w", [PART, 2, 2 * H], U8)
         nc.sync.dma_start(out=w1_w[:].bitcast(I32), in_=w1_words.rearrange("a p c -> p a c").bitcast(I32))
-        load_gate(2)
-        load_gate(3)
         w4_raw = [load_rows(w4[PASS * b : PASS * (b + 1), :]) for b in range(halves)]
-        for s in range(4, len(slices)):
-            load_gate(s)
+
+        def second_plane(first, second):
+            for q in range(4):
+                nc.sync.dma_start(out=second[QUAD * q : QUAD * q + 4, :].bitcast(I32), in_=first[QUAD * q + 4 : QUAD * q + 8, :].bitcast(I32))
+            return [first, second]
+
+        v_s0 = held("v_s0", [PART, S], U8)
+        nc.vector.tensor_copy(v_s0[:], tab_s[:].indirect(idx[:]))
+        v_s = second_plane(v_s0, v_s1)
+        w1_sd0 = held("w1_sd0", [PART, H], U8)
+        nc.vector.tensor_copy(
+            w1_sd0[:].rearrange("p (b t q) -> p b t q", b=halves, t=PACK),
+            w1_s[:].rearrange("p (b q t) -> p b t q", b=halves, t=PACK),
+        )
+        w1_sd = second_plane(w1_sd0, w1_sd1)
 
         v2_w = held("v2_w", [PART, P], U32)
         v2_s = held("v2_s", [PART, P], U8)
@@ -150,9 +166,10 @@ def tile_list_crate_freshness_scores_kernel(
 
         w3_wd = [deal_w3(0)]
 
-        def quantised(name, grouped, width):
+        def quantised(name, grouped, width, scales=None):
             codes = held(name + "_c", [PART, width], U32)
-            scales = held(name + "_s", [PART, width], U8)
+            if scales is None:
+                scales = held(name + "_s", [PART, width], U8)
             nc.vector.quantize_mx(out=codes[:].bitcast(FP8X4), scales=scales[:], in_=grouped)
             return codes, scales
 
@@ -169,8 +186,8 @@ def tile_list_crate_freshness_scores_kernel(
                     made.append((codes[:, PART * t : PART * (t + 1)], scales[:, PART * t : PART * (t + 1)]))
             return made
 
-        def sine_plus_one(arg, turned):
-            wave = ring.tile([PART, P], F32, name="wave", tag="wave" if turned else "wave_first", bufs=2 if turned else 1)
+        def sine_plus_one(arg):
+            wave = ring.tile([PART, P], F32, name="wave", tag="wave", bufs=2)
             nc.scalar.activation(wave[:], arg, ACT.Sin, bias=sin_bias[:], scale=0.25)
             nc.scalar.activation(wave[:], wave[:], ACT.Square)
             nc.scalar.activation(wave[:], wave[:], ACT.Square, bias=root2[:], scale=-2.0 * math.sqrt(2.0))
@@ -193,13 +210,17 @@ def tile_list_crate_freshness_scores_kernel(
                 )
             return bank
 
+        smell_halves = []
+
         def smell_of(s, w2q):
             b, t = slices[s]
-            turned = s >= TURN_FROM
+            turned = s > 0
             w3_part = (w3_wd[b][:, PART * t : PART * (t + 1)], w3_sd[:, PART * s : PART * (s + 1)])
-            wave = sine_plus_one(product("arg", w3_part, turned)[:], turned)
+            wave = sine_plus_one(product("arg", w3_part, turned)[:])
             lin = product("lin", w2q[t], turned)
-            smell = shared.tile([PART, P], F32, name="smell%d" % s, offset=SMELL_AT + 4 * P * s)
+            if t == 0:
+                smell_halves.append(shared.tile([PART, PACK, P], F32, name="smell%d" % b, offset=(FIRST_AT, SECOND_AT)[b]))
+            smell = smell_halves[b][:, t, :]
             if not turned:
                 nc.vector.scalar_tensor_tensor(smell[:], wave[:], -1.0, lin[:], ALU.add, ALU.add)
                 return smell
@@ -211,6 +232,7 @@ def tile_list_crate_freshness_scores_kernel(
                 nc.tensor.matmul(total[:, cols], lhsT=lin_out[:, cols], rhs=ident[:], is_transpose=True, start=True, stop=False)
                 nc.tensor.matmul(total[:, cols], lhsT=wave[:, cols], rhs=ident[:], is_transpose=True, start=False, stop=True)
             nc.scalar.activation(smell[:], total[:], ACT.Copy, bias=-1.0)
+            nc.gpsimd.tensor_tensor(smell[:], smell[:], wg[:, t, :], ALU.mult)
             return smell
 
         def deal_w1(b):
@@ -224,37 +246,29 @@ def tile_list_crate_freshness_scores_kernel(
         w2q = [w2_half(0, w2_first, nc.vector.tensor_copy, ((0, 1), (1, 4)))]
         nc.vector.tensor_copy(w3_sd_view[:, 0, 1:, :], w3_s_view[:, 0, 1:, :])
         nc.vector.tensor_copy(w3_sd_view[:, 1, :, :], w3_s_view[:, 1, :, :])
-        for s, (b, t) in enumerate(slices):
-            if s == 3:
+        smells = []
+        for step in range(len(slices) + AHEAD):
+            if step == PACK - 1:
                 w3_wd.append(deal_w3(1))
-                w2q.append(w2_half(1, [w2_second], nc.scalar.copy, ((0, 4),)))
-            smell = smell_of(s, w2q[b])
-            page = pages[s % PAGES]
-            nc.vector.tensor_tensor(page[:].indirect(places[:]), smell[:], wg[:, t, :], ALU.mult)
-            if s < len(slices) - 1:
-                nc.vector.tensor_tensor(gate[s][:], page[:], gate[s][:], ALU.mult)
+                w2q.append(w2_half(1, [w2_second[:, :, 0 : PASS // 2], w2_second[:, :, PASS // 2 : PASS]], nc.scalar.copy, ((0, 4),)))
+            if step < len(slices):
+                smells.append(smell_of(step, w2q[slices[step][0]]))
+            s = step - AHEAD
+            if s >= 0:
+                page = pages[s % PAGES]
+                if s == 0:
+                    nc.vector.tensor_tensor(page[:].indirect(places[:]), smells[s][:], wg[:, 0, :], ALU.mult)
+                else:
+                    nc.vector.tensor_copy(page[:].indirect(places[:]), smells[s][:])
+                nc.gpsimd.tensor_tensor(gate[s][:], page[:], gate[s][:], ALU.mult)
         w1_wd = [deal_w1(b) for b in range(halves)]
 
-        def second_plane(first, second):
-            for q in range(4):
-                nc.sync.dma_start(out=second[QUAD * q : QUAD * q + 4, :].bitcast(I32), in_=first[QUAD * q + 4 : QUAD * q + 8, :].bitcast(I32))
-            return [first, second]
-
-        v_s0 = held("v_s0", [PART, S], U8)
-        nc.vector.tensor_copy(v_s0[:], tab_s[:].indirect(idx[:]))
-        v_s = second_plane(v_s0, v_s1)
-        w1_sd0 = held("w1_sd0", [PART, H], U8)
-        nc.vector.tensor_copy(
-            w1_sd0[:].rearrange("p (b t q) -> p b t q", b=halves, t=PACK),
-            w1_s[:].rearrange("p (b q t) -> p b t q", b=halves, t=PACK),
-        )
-        w1_sd = second_plane(w1_sd0, w1_sd1)
         v_w = []
         for a in range(2):
             vw = held("v_w%d" % a, [PART, S], U32)
             nc.vector.tensor_copy(vw[:], tab_w[a][:].indirect(idx[:]))
             v_w.append(vw)
-        w4q = []
+        w4_grouped = []
         for b in range(halves):
             grouped = ring.tile([PART, PACK * BANK], BF16, name="grouped", tag="grouped", align_bytes=64)
             for u in range(2):
@@ -262,21 +276,22 @@ def tile_list_crate_freshness_scores_kernel(
                     grouped[:, u * 2 * BANK : (u + 1) * 2 * BANK].rearrange("p (c e i) -> p c i e", e=4, i=PACK),
                     w4_raw[b][:, :, u * BANK // 2 : (u + 1) * BANK // 2].rearrange("p i (c e) -> p c i e", e=4),
                 )
-            w4q.append(quantised("w4q%d" % b, grouped[:], N))
+            w4_grouped.append(grouped)
+        w4q = []
 
         out_rows = out.rearrange("(g p) j -> p g j", p=PART)
-        img_banks = ["arg", "lin", "total", "img0", "img1", "img2"]
+        img_banks = ["free0", "free1", "free2", "free3", "free4", "arg", "lin", "total"]
 
-        def make_z(b, c0, width, copy):
+        def next_bank(per_bank, width):
+            tag = img_banks.pop(0)
+            img_banks.append(tag)
+            return psum.tile([PART, per_bank, width], F32, name="bank", tag=tag, bufs=1)
+
+        def make_z(b, c0, width, z, copy):
             cols = slice(c0, c0 + width)
             per_bank = BANK // width
-            if b == halves - 1 and c0 == 0:
-                nc.vector.tensor_tensor(gate[-1][:], pages[(len(slices) - 1) % PAGES][:], gate[-1][:], ALU.mult)
-            z = ring.tile([PART, PACK, width], BF16, name="z", tag="z", bufs=4)
             for t0 in range(0, PACK, per_bank):
-                tag = img_banks.pop(0)
-                img_banks.append(tag)
-                img = psum.tile([PART, per_bank, width], F32, name="img", tag=tag, bufs=1)
+                img = next_bank(per_bank, width)
                 for u in range(per_bank):
                     r0 = PART * (t0 + u)
                     for a in range(2):
@@ -291,22 +306,33 @@ def tile_list_crate_freshness_scores_kernel(
                     nc.vector.scalar_tensor_tensor(
                         z[:, t, :], img[:, u, :], caps[:, b, t : t + 1], gate[PACK * b + t][:, cols], ALU.min, ALU.add
                     )
-            zg = ring.tile([PART, PACK * width], BF16, name="zg", tag="zg", bufs=4, align_bytes=64)
-            copy(zg[:].rearrange("p (c e t) -> p c t e", e=4, t=PACK), z[:].rearrange("p t (c e) -> p c t e", e=4))
+            zg = ring.tile([PART, PACK * width], BF16, name="zg", tag="zg%d" % b, bufs=2 + b, align_bytes=64)
+            piece = min(width, BANK // 2)
+            for j0 in range(0, width, piece):
+                copy(
+                    zg[:, PACK * j0 : PACK * (j0 + piece)].rearrange("p (c e t) -> p c t e", e=4, t=PACK),
+                    z[:, :, j0 : j0 + piece].rearrange("p t (c e) -> p c t e", e=4),
+                )
             return zg
 
+        first_grouped = []
+        zq_first = []
+
         def finish(c0, width, grouped):
-            zq = [quantised("zq%d_%d" % (c0, b), grouped[b][:], width) for b in range(halves)]
+            codes, scales = zq_first[c0 // BANK]
+            inner = slice(c0 % BANK, c0 % BANK + width)
+            second = quantised("zq_second%d" % c0, grouped[:], width)
+            zq = [(codes[:, inner], scales[:, inner]), (second[0][:], second[1][:])]
             per_bank = BANK // width
-            staged = ring.tile([PART, N // PART, width], F32, name="staged", tag="staged", bufs=3)
+            staged = shared.tile([PART, N // PART, width], F32, name="staged%d" % c0, offset=4 * (N // PART) * c0)
             for g0 in range(0, N // PART, per_bank):
-                acc = psum.tile([PART, per_bank, width], F32, name="acc", tag="acc", bufs=2)
+                acc = next_bank(per_bank, width)
                 for u in range(per_bank):
                     rows = slice(PART * (g0 + u), PART * (g0 + u + 1))
                     for b in range(halves):
                         nc.tensor.matmul_mx(
                             out=acc[:, u, :], lhsT=w4q[b][0][:, rows].bitcast(FP8X4), lhsT_scale=w4q[b][1][:, rows],
-                            rhs=zq[b][0][:].bitcast(FP8X4), rhs_scale=zq[b][1][:],
+                            rhs=zq[b][0].bitcast(FP8X4), rhs_scale=zq[b][1],
                             start=(b == 0), stop=(b == halves - 1),
                         )
                 nc.scalar.copy(staged[:, g0 : g0 + per_bank, :], acc[:])
@@ -315,9 +341,18 @@ def tile_list_crate_freshness_scores_kernel(
         starts = [sum(CHUNKS[:i]) for i in range(len(CHUNKS))]
         waiting = None
         for c0, width in zip(starts, CHUNKS):
-            final = c0 == starts[-1]
-            grouped = [make_z(b, c0, width, nc.vector.tensor_copy if final and b == halves - 1 else nc.scalar.copy) for b in range(halves)]
+            if c0 % BANK == 0:
+                first_grouped.append(make_z(0, c0, BANK, ring.tile([PART, PACK, BANK], BF16, name="z", tag="z_first"), nc.scalar.copy))
+            z = shared.tile([PART, PACK, width], BF16, name="z_second%d" % c0, offset=SECOND_AT + 2 * PACK * c0)
+            grouped = make_z(1, c0, width, z, nc.vector.tensor_copy if c0 >= starts[-2] else nc.scalar.copy)
+            if c0 == 0:
+                w4q.extend(quantised("w4q%d" % b, w4_grouped[b][:], N) for b in range(halves))
+            if c0 % BANK == 0:
+                zq_first.append(quantised("zq_first%d" % c0, first_grouped[c0 // BANK][:], BANK))
             if waiting is not None:
                 finish(*waiting)
             waiting = (c0, width, grouped)
+            if c0 == 0:
+                finish(*waiting)
+                waiting = None
         finish(*waiting)

@@ -22,12 +22,19 @@ PART = 128
 PACK = 4
 PASS = PART * PACK
 QUAD = 32
+QUADS = PART // QUAD
+LIVE = 4
+GROUP = 16
 BANK = 512
+RUN = 4
 PAGES = 3
 AHEAD = 2
-FIRST_AT = 4 * PACK * P
-SECOND_AT = 2 * FIRST_AT
 CHUNKS = (256, 256, 256, 128, 128)
+NARROW = 2
+ROW_BYTES = 4 * P
+REGION = PACK * ROW_BYTES
+FIRST_AT = REGION
+SECOND_AT = 2 * REGION
 
 
 def tile_list_crate_freshness_scores_kernel(
@@ -68,24 +75,26 @@ def tile_list_crate_freshness_scores_kernel(
         for plane in (tab_s, w1_s, v_s1, w1_sd1):
             nc.vector.memset(plane[:].bitcast(I32), 0)
 
-        def load_plane(queue, plane, rows):
-            for q in range(4):
-                queue.dma_start(
+        def load_plane(plane, rows):
+            for q in range(QUADS):
+                nc.sync.dma_start(
                     out=plane[QUAD * q : QUAD * (q + 1), :].bitcast(I32),
-                    in_=rows[4 * q : 4 * q + 4, :].bitcast(I32).partition_broadcast(QUAD // 4),
+                    in_=rows[LIVE * q : LIVE * (q + 1), :].bitcast(I32).partition_broadcast(QUAD // LIVE),
                 )
 
-        idx2 = held("idx2", [PART, P // 16], U16)
+        idx2 = held("idx2", [PART, P // GROUP], U16)
         nc.sync.dma_start(out=idx2[:], in_=offs2)
-        load_plane(nc.sync, tab2_s, tab2_scales[0])
+        wg_rows = held("wg_rows", [PART, P], F32)
+        nc.sync.dma_start(out=wg_rows[:], in_=wgs)
+        load_plane(tab2_s, tab2_scales[0])
         tab2_w = held("tab2_w", [PART, T3], U32)
         nc.sync.dma_start(out=tab2_w[:].bitcast(I32), in_=tab2_words[0].rearrange("p t i -> p (t i)").bitcast(I32))
         w3_rows = w3_words[0].rearrange("p c i -> p (c i)").bitcast(I32)
         w3_w = [held("w3_w%d" % b, [PART, PASS], U32) for b in range(halves)]
         nc.sync.dma_start(out=w3_w[0][:].bitcast(I32), in_=w3_rows[:, 0:PASS])
-        load_plane(nc.sync, w3_s, w3_scales[0])
+        load_plane(w3_s, w3_scales[0])
         w2_first = [
-            shared.tile([PART, PACK, PASS // 2], F32, name="w2_first%d" % u, offset=SECOND_AT + u * FIRST_AT // 2) for u in range(2)
+            shared.tile([PART, PACK, PASS // 2], F32, name="w2_first%d" % u, offset=(SECOND_AT, ROW_BYTES)[u]) for u in range(2)
         ]
         for u in range(2):
             nc.sync.dma_start(out=w2_first[u][:], in_=w2[:, u * PASS // 2 : (u + 1) * PASS // 2].rearrange("(p i) c -> p i c", i=PACK))
@@ -96,49 +105,49 @@ def tile_list_crate_freshness_scores_kernel(
             return raw
 
         def load_two_planes(plane, rows):
-            for q in range(4):
-                nc.sync.dma_start(out=plane[QUAD * q : QUAD * q + 8, :].bitcast(I32), in_=rows[:, 4 * q : 4 * q + 4, :].bitcast(I32))
+            for q in range(QUADS):
+                nc.sync.dma_start(
+                    out=plane[QUAD * q : QUAD * q + 2 * LIVE, :].bitcast(I32), in_=rows[:, LIVE * q : LIVE * (q + 1), :].bitcast(I32)
+                )
 
-        places = held("places", [PART, P // 16], U16)
+        places = held("places", [PART, P // GROUP], U16)
         nc.sync.dma_start(out=places[:], in_=pos1)
-        wg = shared.tile([PART, PACK, P], F32, name="wg", offset=0)
-        for q in range(4):
-            nc.sync.dma_start(out=wg[QUAD * q : QUAD * (q + 1), :, :], in_=wgs.rearrange("(p t) j -> p t j", t=PACK))
         gm_rows = gm.rearrange("(b p t) j -> b t p j", b=halves, t=PACK)
         gate = [held("gate%d" % s, [PART, S], F32) for s in range(len(slices))]
 
-        def load_gate(s):
-            b, t = slices[s]
-            nc.sync.dma_start(out=gate[s][:], in_=gm_rows[b, t])
+        def load_gates(first, end):
+            for s in range(first, end):
+                b, t = slices[s]
+                nc.sync.dma_start(out=gate[s][:], in_=gm_rows[b, t])
 
         tab_w = [held("tab_w%d" % a, [PART, T], U32) for a in range(2)]
 
         def load_tab(a):
             nc.sync.dma_start(out=tab_w[a][:].bitcast(I32), in_=tab_words[a].rearrange("p t i -> p (t i)").bitcast(I32))
 
-        idx = held("idx", [PART, S // 16], U16)
+        w2_second = load_rows(w2[:, PASS : 2 * PASS])
+        idx = held("idx", [PART, S // GROUP], U16)
         nc.sync.dma_start(out=idx[:], in_=offs)
         load_two_planes(tab_s, tab_scales)
-        w2_second = load_rows(w2[:, PASS : 2 * PASS])
         nc.sync.dma_start(out=w3_w[1][:].bitcast(I32), in_=w3_rows[:, PASS : 2 * PASS])
         caps = held("caps", [PART, halves, PACK], F32)
         nc.sync.dma_start(out=caps[:], in_=cap.rearrange("(b p t) -> p b t", b=halves, t=PACK))
-        for s in range(4):
-            if s == 3:
-                load_two_planes(w1_s, w1_scales)
-            load_gate(s)
+        load_gates(0, PAGES - 1)
+        load_two_planes(w1_s, w1_scales)
         load_tab(0)
-        for s in range(4, len(slices)):
-            load_gate(s)
+        load_gates(PAGES - 1, len(slices))
         load_tab(1)
         w1_w = held("w1_w", [PART, 2, 2 * H], U8)
         nc.sync.dma_start(out=w1_w[:].bitcast(I32), in_=w1_words.rearrange("a p c -> p a c").bitcast(I32))
         w4_raw = [load_rows(w4[PASS * b : PASS * (b + 1), :]) for b in range(halves)]
 
-        def second_plane(first, second):
-            for q in range(4):
-                nc.sync.dma_start(out=second[QUAD * q : QUAD * q + 4, :].bitcast(I32), in_=first[QUAD * q + 4 : QUAD * q + 8, :].bitcast(I32))
-            return [first, second]
+        def second_plane(both, second):
+            for q in range(QUADS):
+                nc.sync.dma_start(
+                    out=second[QUAD * q : QUAD * q + LIVE, :].bitcast(I32),
+                    in_=both[QUAD * q + LIVE : QUAD * q + 2 * LIVE, :].bitcast(I32),
+                )
+            return [both, second]
 
         v_s0 = held("v_s0", [PART, S], U8)
         nc.vector.tensor_copy(v_s0[:], tab_s[:].indirect(idx[:]))
@@ -150,6 +159,27 @@ def tile_list_crate_freshness_scores_kernel(
         )
         w1_sd = second_plane(w1_sd0, w1_sd1)
 
+        quarters = P // PART
+        wg_bank = psum.tile([PART, quarters, PART], F32, name="wg_bank", tag="free0", bufs=1)
+        wg_turned = held("wg_turned", [PART, quarters, PACK * PART], F32)
+        for u in range(quarters):
+            nc.tensor.transpose(wg_bank[:, u, :], wg_rows[:, PART * u : PART * (u + 1)], ident[:])
+        for u in range(quarters):
+            nc.scalar.copy(
+                wg_turned[:, u, :].rearrange("p (t g q) -> p t g q", t=PACK, q=QUAD),
+                wg_bank[:, u, :].rearrange("p (q t) -> p t q", t=PACK).unsqueeze(2).to_broadcast([PART, PACK, QUADS, QUAD]),
+            )
+
+        def deal_wgs(t):
+            bank = psum.tile([PART, P], F32, name="wg_dealt", tag="free%d" % (t + 1), bufs=1)
+            for u in range(quarters):
+                nc.tensor.transpose(bank[:, PART * u : PART * (u + 1)], wg_turned[:, u, PART * t : PART * (t + 1)], ident[:])
+            nc.scalar.copy(wg[t], bank[:])
+
+        wg_first = shared.tile([PART, P], F32, name="wg_first", offset=0)
+        wg = [wg_first[:]]
+        deal_wgs(0)
+
         v2_w = held("v2_w", [PART, P], U32)
         v2_s = held("v2_s", [PART, P], U8)
         nc.vector.tensor_copy(v2_s[:], tab2_s[:].indirect(idx2[:]))
@@ -160,16 +190,15 @@ def tile_list_crate_freshness_scores_kernel(
         nc.vector.tensor_copy(w3_sd_view[:, 0, 0, :], w3_s_view[:, 0, 0, :])
 
         def deal_w3(b):
-            wd = held("w3_wd%d" % b, [PART, PASS], U32)
-            nc.scalar.copy(wd[:].rearrange("p (t q) -> p t q", t=PACK), w3_w[b][:].rearrange("p (q t) -> p t q", t=PACK))
-            return wd
+            dealt = held("w3_wd%d" % b, [PART, PASS], U32)
+            nc.scalar.copy(dealt[:].rearrange("p (t q) -> p t q", t=PACK), w3_w[b][:].rearrange("p (q t) -> p t q", t=PACK))
+            return dealt
 
         w3_wd = [deal_w3(0)]
 
-        def quantised(name, grouped, width, scales=None):
+        def quantised(name, grouped, width):
             codes = held(name + "_c", [PART, width], U32)
-            if scales is None:
-                scales = held(name + "_s", [PART, width], U8)
+            scales = held(name + "_s", [PART, width], U8)
             nc.vector.quantize_mx(out=codes[:].bitcast(FP8X4), scales=scales[:], in_=grouped)
             return codes, scales
 
@@ -187,7 +216,7 @@ def tile_list_crate_freshness_scores_kernel(
             return made
 
         def sine_plus_one(arg):
-            wave = ring.tile([PART, P], F32, name="wave", tag="wave", bufs=2)
+            wave = ring.tile([PART, P], F32, name="wave", tag="wave")
             nc.scalar.activation(wave[:], arg, ACT.Sin, bias=sin_bias[:], scale=0.25)
             nc.scalar.activation(wave[:], wave[:], ACT.Square)
             nc.scalar.activation(wave[:], wave[:], ACT.Square, bias=root2[:], scale=-2.0 * math.sqrt(2.0))
@@ -212,19 +241,19 @@ def tile_list_crate_freshness_scores_kernel(
 
         smell_halves = []
 
-        def smell_of(s, w2q):
+        def smell_of(s, w2_parts):
             b, t = slices[s]
             turned = s > 0
             w3_part = (w3_wd[b][:, PART * t : PART * (t + 1)], w3_sd[:, PART * s : PART * (s + 1)])
             wave = sine_plus_one(product("arg", w3_part, turned)[:])
-            lin = product("lin", w2q[t], turned)
+            lin = product("lin", w2_parts[t], turned)
             if t == 0:
                 smell_halves.append(shared.tile([PART, PACK, P], F32, name="smell%d" % b, offset=(FIRST_AT, SECOND_AT)[b]))
             smell = smell_halves[b][:, t, :]
             if not turned:
                 nc.vector.scalar_tensor_tensor(smell[:], wave[:], -1.0, lin[:], ALU.add, ALU.add)
                 return smell
-            lin_out = ring.tile([PART, P], F32, name="lin_out", tag="lin_out", bufs=2)
+            lin_out = ring.tile([PART, P], F32, name="lin_out", tag="lin_out")
             nc.scalar.copy(lin_out[:], lin[:])
             total = psum.tile([PART, P], F32, name="total", tag="total", bufs=1)
             for j0 in range(0, P, PART):
@@ -232,32 +261,38 @@ def tile_list_crate_freshness_scores_kernel(
                 nc.tensor.matmul(total[:, cols], lhsT=lin_out[:, cols], rhs=ident[:], is_transpose=True, start=True, stop=False)
                 nc.tensor.matmul(total[:, cols], lhsT=wave[:, cols], rhs=ident[:], is_transpose=True, start=False, stop=True)
             nc.scalar.activation(smell[:], total[:], ACT.Copy, bias=-1.0)
-            nc.gpsimd.tensor_tensor(smell[:], smell[:], wg[:, t, :], ALU.mult)
+            nc.gpsimd.tensor_tensor(smell[:], smell[:], wg[t], ALU.mult)
             return smell
 
         def deal_w1(b):
-            wd = held("w1_wd%d" % b, [PART, 2, 2 * PASS], U8)
+            dealt = held("w1_wd%d" % b, [PART, 2, 2 * PASS], U8)
             nc.scalar.copy(
-                wd[:].bitcast(U16).rearrange("p a (t q) -> p a t q", t=PACK),
+                dealt[:].bitcast(U16).rearrange("p a (t q) -> p a t q", t=PACK),
                 w1_w[:, :, 2 * PASS * b : 2 * PASS * (b + 1)].bitcast(U16).rearrange("p a (q t) -> p a t q", t=PACK),
             )
-            return wd
+            return dealt
 
-        w2q = [w2_half(0, w2_first, nc.vector.tensor_copy, ((0, 1), (1, 4)))]
+        w2q = [w2_half(0, w2_first, nc.vector.tensor_copy, ((0, 1), (1, PACK)))]
         nc.vector.tensor_copy(w3_sd_view[:, 0, 1:, :], w3_s_view[:, 0, 1:, :])
         nc.vector.tensor_copy(w3_sd_view[:, 1, :, :], w3_s_view[:, 1, :, :])
+
         smells = []
         for step in range(len(slices) + AHEAD):
+            if step == 1:
+                wg_rest = shared.tile([PART, PACK - 1, P], F32, name="wg_rest", offset=ROW_BYTES)
+                wg.extend(wg_rest[:, t, :] for t in range(PACK - 1))
+                for t in range(1, PACK):
+                    deal_wgs(t)
             if step == PACK - 1:
                 w3_wd.append(deal_w3(1))
-                w2q.append(w2_half(1, [w2_second[:, :, 0 : PASS // 2], w2_second[:, :, PASS // 2 : PASS]], nc.scalar.copy, ((0, 4),)))
+                w2q.append(w2_half(1, [w2_second[:, :, 0 : PASS // 2], w2_second[:, :, PASS // 2 : PASS]], nc.scalar.copy, ((0, PACK),)))
             if step < len(slices):
                 smells.append(smell_of(step, w2q[slices[step][0]]))
             s = step - AHEAD
             if s >= 0:
                 page = pages[s % PAGES]
                 if s == 0:
-                    nc.vector.tensor_tensor(page[:].indirect(places[:]), smells[s][:], wg[:, 0, :], ALU.mult)
+                    nc.vector.tensor_tensor(page[:].indirect(places[:]), smells[s][:], wg[0], ALU.mult)
                 else:
                     nc.vector.tensor_copy(page[:].indirect(places[:]), smells[s][:])
                 nc.gpsimd.tensor_tensor(gate[s][:], page[:], gate[s][:], ALU.mult)
@@ -265,26 +300,26 @@ def tile_list_crate_freshness_scores_kernel(
 
         v_w = []
         for a in range(2):
-            vw = held("v_w%d" % a, [PART, S], U32)
-            nc.vector.tensor_copy(vw[:], tab_w[a][:].indirect(idx[:]))
-            v_w.append(vw)
+            words = held("v_w%d" % a, [PART, S], U32)
+            nc.vector.tensor_copy(words[:], tab_w[a][:].indirect(idx[:]))
+            v_w.append(words)
         w4_grouped = []
         for b in range(halves):
             grouped = ring.tile([PART, PACK * BANK], BF16, name="grouped", tag="grouped", align_bytes=64)
             for u in range(2):
                 nc.scalar.copy(
-                    grouped[:, u * 2 * BANK : (u + 1) * 2 * BANK].rearrange("p (c e i) -> p c i e", e=4, i=PACK),
-                    w4_raw[b][:, :, u * BANK // 2 : (u + 1) * BANK // 2].rearrange("p i (c e) -> p c i e", e=4),
+                    grouped[:, u * 2 * BANK : (u + 1) * 2 * BANK].rearrange("p (c e i) -> p c i e", e=RUN, i=PACK),
+                    w4_raw[b][:, :, u * BANK // 2 : (u + 1) * BANK // 2].rearrange("p i (c e) -> p c i e", e=RUN),
                 )
             w4_grouped.append(grouped)
         w4q = []
 
         out_rows = out.rearrange("(g p) j -> p g j", p=PART)
-        img_banks = ["free0", "free1", "free2", "free3", "free4", "arg", "lin", "total"]
+        bank_tags = ["free0", "free1", "free2", "free3", "free4", "arg", "lin", "total"]
 
         def next_bank(per_bank, width):
-            tag = img_banks.pop(0)
-            img_banks.append(tag)
+            tag = bank_tags.pop(0)
+            bank_tags.append(tag)
             return psum.tile([PART, per_bank, width], F32, name="bank", tag=tag, bufs=1)
 
         def make_z(b, c0, width, z, copy):
@@ -306,22 +341,22 @@ def tile_list_crate_freshness_scores_kernel(
                     nc.vector.scalar_tensor_tensor(
                         z[:, t, :], img[:, u, :], caps[:, b, t : t + 1], gate[PACK * b + t][:, cols], ALU.min, ALU.add
                     )
-            zg = ring.tile([PART, PACK * width], BF16, name="zg", tag="zg%d" % b, bufs=2 + b, align_bytes=64)
-            piece = min(width, BANK // 2)
+            regrouped = ring.tile([PART, PACK * width], BF16, name="zg", tag="zg%d" % b, bufs=2 + b, align_bytes=64)
+            piece = min(width, CHUNKS[0])
             for j0 in range(0, width, piece):
                 copy(
-                    zg[:, PACK * j0 : PACK * (j0 + piece)].rearrange("p (c e t) -> p c t e", e=4, t=PACK),
-                    z[:, :, j0 : j0 + piece].rearrange("p t (c e) -> p c t e", e=4),
+                    regrouped[:, PACK * j0 : PACK * (j0 + piece)].rearrange("p (c e t) -> p c t e", e=RUN, t=PACK),
+                    z[:, :, j0 : j0 + piece].rearrange("p t (c e) -> p c t e", e=RUN),
                 )
-            return zg
+            return regrouped
 
-        first_grouped = []
+        first_regrouped = []
         zq_first = []
 
-        def finish(c0, width, grouped):
+        def finish(c0, width, regrouped):
             codes, scales = zq_first[c0 // BANK]
             inner = slice(c0 % BANK, c0 % BANK + width)
-            second = quantised("zq_second%d" % c0, grouped[:], width)
+            second = quantised("zq_second%d" % c0, regrouped[:], width)
             zq = [(codes[:, inner], scales[:, inner]), (second[0][:], second[1][:])]
             per_bank = BANK // width
             staged = shared.tile([PART, N // PART, width], F32, name="staged%d" % c0, offset=4 * (N // PART) * c0)
@@ -342,16 +377,17 @@ def tile_list_crate_freshness_scores_kernel(
         waiting = None
         for c0, width in zip(starts, CHUNKS):
             if c0 % BANK == 0:
-                first_grouped.append(make_z(0, c0, BANK, ring.tile([PART, PACK, BANK], BF16, name="z", tag="z_first"), nc.scalar.copy))
-            z = shared.tile([PART, PACK, width], BF16, name="z_second%d" % c0, offset=SECOND_AT + 2 * PACK * c0)
-            grouped = make_z(1, c0, width, z, nc.vector.tensor_copy if c0 >= starts[-2] else nc.scalar.copy)
+                z_first = ring.tile([PART, PACK, BANK], BF16, name="z", tag="z_first")
+                first_regrouped.append(make_z(0, c0, BANK, z_first, nc.scalar.copy))
+            z_second = shared.tile([PART, PACK, width], BF16, name="z_second%d" % c0, offset=SECOND_AT + 2 * PACK * c0)
+            regrouped = make_z(1, c0, width, z_second, nc.vector.tensor_copy if c0 >= starts[-NARROW] else nc.scalar.copy)
             if c0 == 0:
                 w4q.extend(quantised("w4q%d" % b, w4_grouped[b][:], N) for b in range(halves))
             if c0 % BANK == 0:
-                zq_first.append(quantised("zq_first%d" % c0, first_grouped[c0 // BANK][:], BANK))
+                zq_first.append(quantised("zq_first%d" % c0, first_regrouped[c0 // BANK][:], BANK))
             if waiting is not None:
                 finish(*waiting)
-            waiting = (c0, width, grouped)
+            waiting = (c0, width, regrouped)
             if c0 == 0:
                 finish(*waiting)
                 waiting = None

import math
from contextlib import ExitStack

import concourse.mybir as mybir
from concourse.masks import make_identity

K, K2, H, N, T, S, T3, P = 1024, 512, 1024, 512, 4096, 1024, 2048, 512
FLOPS = 2 * (K * H * S + 2 * K2 * H * P + H * N * S)

F32 = mybir.dt.float32
BF16 = mybir.dt.bfloat16
I32 = mybir.dt.int32
U32 = mybir.dt.uint32
U16 = mybir.dt.uint16
U8 = mybir.dt.uint8
FP8X4 = mybir.dt.float8_e4m3fn_x4
FP4X4 = mybir.dt.float4_e2m1fn_x4
ALU = mybir.AluOpType
ACT = mybir.ActivationFunctionType

PART = 128
PACK = 4
PASS = PART * PACK
QUAD = 32
QUADS = PART // QUAD
LIVE = 4
GROUP = 16
BANK = 512
RUN = 4
PAGES = 3
AHEAD = 2
CHUNKS = (256, 256, 256, 128, 128)
NARROW = 2
ROW_BYTES = 4 * P
REGION = PACK * ROW_BYTES
FIRST_AT = REGION
SECOND_AT = 2 * REGION


def tile_list_crate_freshness_scores_kernel(
    tc, tab_words, tab_scales, tab2_words, tab2_scales, offs, offs2, pos1, w1_words, w1_scales,
    cap, w2, w3_words, w3_scales, wgs, gm, w4, out,
):
    nc = tc.nc
    halves = H // PASS
    slices = [(b, t) for b in range(halves) for t in range(PACK)]

    with ExitStack() as ctx:
        keep = ctx.enter_context(tc.tile_pool(name="keep", bufs=1))
        ring = ctx.enter_context(tc.tile_pool(name="ring", bufs=2))
        shared = ctx.enter_context(tc.tile_pool(name="shared", bufs=1))
        psum = ctx.enter_context(tc.psum_pool(name="psum", bufs=1))

        def held(name, shape, dtype):
            return keep.tile(shape, dtype, name=name, align_bytes=64)

        tab2_s = held("tab2_s", [PART, T3], U8)
        w3_s = held("w3_s", [PART, H], U8)
        w1_s = held("w1_s", [PART, H], U8)
        w1_sd1 = held("w1_sd1", [PART, H], U8)
        tab_s = held("tab_s", [PART, T], U8)
        v_s1 = held("v_s1", [PART, S], U8)
        one = held("one", [PART, 1], F32)
        sin_bias = held("sin_bias", [PART, 1], F32)
        root2 = held("root2", [PART, 1], F32)
        nc.vector.memset(one[:], 1.0)
        nc.vector.tensor_scalar(sin_bias[:], one[:], -math.pi / 8, None, ALU.mult)
        nc.scalar.activation(root2[:], one[:], ACT.Sin, scale=math.pi / 4)
        nc.vector.tensor_scalar(root2[:], root2[:], 2.0, None, ALU.mult)
        ident = held("ident", [PART, PART], F32)
        make_identity(nc, ident[:])
        pages = [held("page%d" % i, [PART, S], F32) for i in range(PAGES)]
        for page in pages:
            nc.vector.memset(page[:], 0.0)
        for plane in (tab_s, w1_s, v_s1, w1_sd1):
            nc.vector.memset(plane[:].bitcast(I32), 0)

        def load_plane(plane, rows):
            for q in range(QUADS):
                nc.sync.dma_start(
                    out=plane[QUAD * q : QUAD * (q + 1), :].bitcast(I32),
                    in_=rows[LIVE * q : LIVE * (q + 1), :].bitcast(I32).partition_broadcast(QUAD // LIVE),
                )

        idx2 = held("idx2", [PART, P // GROUP], U16)
        nc.sync.dma_start(out=idx2[:], in_=offs2)
        wg_rows = held("wg_rows", [PART, P], F32)
        nc.sync.dma_start(out=wg_rows[:], in_=wgs)
        load_plane(tab2_s, tab2_scales[0])
        tab2_w = held("tab2_w", [PART, T3], U32)
        nc.sync.dma_start(out=tab2_w[:].bitcast(I32), in_=tab2_words[0].rearrange("p t i -> p (t i)").bitcast(I32))
        w3_rows = w3_words[0].rearrange("p c i -> p (c i)").bitcast(I32)
        w3_w = [held("w3_w%d" % b, [PART, PASS], U32) for b in range(halves)]
        nc.sync.dma_start(out=w3_w[0][:].bitcast(I32), in_=w3_rows[:, 0:PASS])
        load_plane(w3_s, w3_scales[0])
        w2_first = [
            shared.tile([PART, PACK, PASS // 2], F32, name="w2_first%d" % u, offset=(SECOND_AT, ROW_BYTES)[u]) for u in range(2)
        ]
        for u in range(2):
            nc.sync.dma_start(out=w2_first[u][:], in_=w2[:, u * PASS // 2 : (u + 1) * PASS // 2].rearrange("(p i) c -> p i c", i=PACK))

        def load_rows(src):
            raw = ring.tile([PART, PACK, BANK], F32, name="raw", tag="raw")
            nc.sync.dma_start(out=raw[:], in_=src.rearrange("(p i) c -> p i c", i=PACK))
            return raw

        def load_two_planes(plane, rows):
            for q in range(QUADS):
                nc.sync.dma_start(
                    out=plane[QUAD * q : QUAD * q + 2 * LIVE, :].bitcast(I32), in_=rows[:, LIVE * q : LIVE * (q + 1), :].bitcast(I32)
                )

        places = held("places", [PART, P // GROUP], U16)
        nc.sync.dma_start(out=places[:], in_=pos1)
        gm_rows = gm.rearrange("(b p t) j -> b t p j", b=halves, t=PACK)
        gate = [held("gate%d" % s, [PART, S], F32) for s in range(len(slices))]

        def load_gates(first, end):
            for s in range(first, end):
                b, t = slices[s]
                nc.sync.dma_start(out=gate[s][:], in_=gm_rows[b, t])

        tab_w = [held("tab_w%d" % a, [PART, T], U32) for a in range(2)]

        def load_tab(a):
            nc.sync.dma_start(out=tab_w[a][:].bitcast(I32), in_=tab_words[a].rearrange("p t i -> p (t i)").bitcast(I32))

        w2_second = load_rows(w2[:, PASS : 2 * PASS])
        idx = held("idx", [PART, S // GROUP], U16)
        nc.sync.dma_start(out=idx[:], in_=offs)
        load_two_planes(tab_s, tab_scales)
        nc.sync.dma_start(out=w3_w[1][:].bitcast(I32), in_=w3_rows[:, PASS : 2 * PASS])
        caps = held("caps", [PART, halves, PACK], F32)
        nc.sync.dma_start(out=caps[:], in_=cap.rearrange("(b p t) -> p b t", b=halves, t=PACK))
        load_gates(0, PAGES - 1)
        load_two_planes(w1_s, w1_scales)
        load_tab(0)
        load_gates(PAGES - 1, len(slices))
        load_tab(1)
        w1_w = held("w1_w", [PART, 2, 2 * H], U8)
        nc.sync.dma_start(out=w1_w[:].bitcast(I32), in_=w1_words.rearrange("a p c -> p a c").bitcast(I32))
        w4_raw = [load_rows(w4[PASS * b : PASS * (b + 1), :]) for b in range(halves)]

        def second_plane(both, second):
            for q in range(QUADS):
                nc.sync.dma_start(
                    out=second[QUAD * q : QUAD * q + LIVE, :].bitcast(I32),
                    in_=both[QUAD * q + LIVE : QUAD * q + 2 * LIVE, :].bitcast(I32),
                )
            return [both, second]

        v_s0 = held("v_s0", [PART, S], U8)
        nc.vector.tensor_copy(v_s0[:], tab_s[:].indirect(idx[:]))
        v_s = second_plane(v_s0, v_s1)
        w1_sd0 = held("w1_sd0", [PART, H], U8)
        nc.vector.tensor_copy(
            w1_sd0[:].rearrange("p (b t q) -> p b t q", b=halves, t=PACK),
            w1_s[:].rearrange("p (b q t) -> p b t q", b=halves, t=PACK),
        )
        w1_sd = second_plane(w1_sd0, w1_sd1)

        quarters = P // PART
        wg_bank = psum.tile([PART, quarters, PART], F32, name="wg_bank", tag="free0", bufs=1)
        wg_turned = held("wg_turned", [PART, quarters, PACK * PART], F32)
        for u in range(quarters):
            nc.tensor.transpose(wg_bank[:, u, :], wg_rows[:, PART * u : PART * (u + 1)], ident[:])
        for u in range(quarters):
            nc.scalar.copy(
                wg_turned[:, u, :].rearrange("p (t g q) -> p t g q", t=PACK, q=QUAD),
                wg_bank[:, u, :].rearrange("p (q t) -> p t q", t=PACK).unsqueeze(2).to_broadcast([PART, PACK, QUADS, QUAD]),
            )

        def deal_wgs(t):
            bank = psum.tile([PART, P], F32, name="wg_dealt", tag="free%d" % (t + 1), bufs=1)
            for u in range(quarters):
                nc.tensor.transpose(bank[:, PART * u : PART * (u + 1)], wg_turned[:, u, PART * t : PART * (t + 1)], ident[:])
            nc.scalar.copy(wg[t], bank[:])

        wg_first = shared.tile([PART, P], F32, name="wg_first", offset=0)
        wg = [wg_first[:]]
        deal_wgs(0)

        v2_w = held("v2_w", [PART, P], U32)
        v2_s = held("v2_s", [PART, P], U8)
        nc.vector.tensor_copy(v2_s[:], tab2_s[:].indirect(idx2[:]))
        nc.vector.tensor_copy(v2_w[:], tab2_w[:].indirect(idx2[:]))
        w3_sd = held("w3_sd", [PART, H], U8)
        w3_sd_view = w3_sd[:].rearrange("p (b t q) -> p b t q", b=halves, t=PACK)
        w3_s_view = w3_s[:].rearrange("p (b q t) -> p b t q", b=halves, t=PACK)
        nc.vector.tensor_copy(w3_sd_view[:, 0, 0, :], w3_s_view[:, 0, 0, :])

        def deal_w3(b):
            dealt = held("w3_wd%d" % b, [PART, PASS], U32)
            nc.scalar.copy(dealt[:].rearrange("p (t q) -> p t q", t=PACK), w3_w[b][:].rearrange("p (q t) -> p t q", t=PACK))
            return dealt

        w3_wd = [deal_w3(0)]

        def quantised(name, grouped, width):
            codes = held(name + "_c", [PART, width], U32)
            scales = held(name + "_s", [PART, width], U8)
            nc.vector.quantize_mx(out=codes[:].bitcast(FP8X4), scales=scales[:], in_=grouped)
            return codes, scales

        def w2_half(b, parts, copy, cuts):
            grouped = ring.tile([PART, PACK * BANK], BF16, name="grouped", tag="grouped", align_bytes=64)
            dealt = grouped[:].rearrange("p (t q i) -> p q t i", t=PACK, i=PACK)
            share = PART // len(parts)
            for u, raw in enumerate(parts):
                copy(dealt[:, share * u : share * (u + 1), :, :], raw[:].rearrange("p i (q t) -> p q t i", t=PACK))
            made = []
            for t0, t1 in cuts:
                codes, scales = quantised("w2q%d_%d" % (b, t0), grouped[:, BANK * t0 : BANK * t1], PART * (t1 - t0))
                for t in range(t1 - t0):
                    made.append((codes[:, PART * t : PART * (t + 1)], scales[:, PART * t : PART * (t + 1)]))
            return made

        def sine_plus_one(arg):
            wave = ring.tile([PART, P], F32, name="wave", tag="wave")
            nc.scalar.activation(wave[:], arg, ACT.Sin, bias=sin_bias[:], scale=0.25)
            nc.scalar.activation(wave[:], wave[:], ACT.Square)
            nc.scalar.activation(wave[:], wave[:], ACT.Square, bias=root2[:], scale=-2.0 * math.sqrt(2.0))
            return wave

        def product(tag, weight, turned):
            bank = psum.tile([PART, P], F32, name=tag, tag=tag, bufs=1)
            codes, scales = weight
            if turned:
                for j0 in range(0, P, PART):
                    cols = slice(j0, j0 + PART)
                    nc.tensor.matmul_mx(
                        out=bank[:, cols], lhsT=v2_w[:, cols].bitcast(FP8X4), lhsT_scale=v2_s[:, cols],
                        rhs=codes.bitcast(FP8X4), rhs_scale=scales, start=True, stop=True,
                    )
            else:
                nc.tensor.matmul_mx(
                    out=bank[:], lhsT=codes.bitcast(FP8X4), lhsT_scale=scales,
                    rhs=v2_w[:].bitcast(FP8X4), rhs_scale=v2_s[:], start=True, stop=True,
                )
            return bank

        smell_halves = []

        def smell_of(s, w2_parts):
            b, t = slices[s]
            turned = s > 0
            w3_part = (w3_wd[b][:, PART * t : PART * (t + 1)], w3_sd[:, PART * s : PART * (s + 1)])
            wave = sine_plus_one(product("arg", w3_part, turned)[:])
            lin = product("lin", w2_parts[t], turned)
            if t == 0:
                smell_halves.append(shared.tile([PART, PACK, P], F32, name="smell%d" % b, offset=(FIRST_AT, SECOND_AT)[b]))
            smell = smell_halves[b][:, t, :]
            if not turned:
                nc.vector.scalar_tensor_tensor(smell[:], wave[:], -1.0, lin[:], ALU.add, ALU.add)
                return smell
            lin_out = ring.tile([PART, P], F32, name="lin_out", tag="lin_out")
            nc.scalar.copy(lin_out[:], lin[:])
            total = psum.tile([PART, P], F32, name="total", tag="total", bufs=1)
            for j0 in range(0, P, PART):
                cols = slice(j0, j0 + PART)
                nc.tensor.matmul(total[:, cols], lhsT=lin_out[:, cols], rhs=ident[:], is_transpose=True, start=True, stop=False)
                nc.tensor.matmul(total[:, cols], lhsT=wave[:, cols], rhs=ident[:], is_transpose=True, start=False, stop=True)
            nc.scalar.activation(smell[:], total[:], ACT.Copy, bias=-1.0)
            nc.gpsimd.tensor_tensor(smell[:], smell[:], wg[t], ALU.mult)
            return smell

        def deal_w1(b):
            dealt = held("w1_wd%d" % b, [PART, 2, 2 * PASS], U8)
            nc.scalar.copy(
                dealt[:].bitcast(U16).rearrange("p a (t q) -> p a t q", t=PACK),
                w1_w[:, :, 2 * PASS * b : 2 * PASS * (b + 1)].bitcast(U16).rearrange("p a (q t) -> p a t q", t=PACK),
            )
            return dealt

        w2q = [w2_half(0, w2_first, nc.vector.tensor_copy, ((0, 1), (1, PACK)))]
        nc.vector.tensor_copy(w3_sd_view[:, 0, 1:, :], w3_s_view[:, 0, 1:, :])
        nc.vector.tensor_copy(w3_sd_view[:, 1, :, :], w3_s_view[:, 1, :, :])

        smells = []
        for step in range(len(slices) + AHEAD):
            if step == 1:
                wg_rest = shared.tile([PART, PACK - 1, P], F32, name="wg_rest", offset=ROW_BYTES)
                wg.extend(wg_rest[:, t, :] for t in range(PACK - 1))
                for t in range(1, PACK):
                    deal_wgs(t)
            if step == PACK - 1:
                w3_wd.append(deal_w3(1))
                w2q.append(w2_half(1, [w2_second[:, :, 0 : PASS // 2], w2_second[:, :, PASS // 2 : PASS]], nc.scalar.copy, ((0, PACK),)))
            if step < len(slices):
                smells.append(smell_of(step, w2q[slices[step][0]]))
            s = step - AHEAD
            if s >= 0:
                page = pages[s % PAGES]
                if s == 0:
                    nc.vector.tensor_tensor(page[:].indirect(places[:]), smells[s][:], wg[0], ALU.mult)
                else:
                    nc.vector.tensor_copy(page[:].indirect(places[:]), smells[s][:])
                nc.gpsimd.tensor_tensor(gate[s][:], page[:], gate[s][:], ALU.mult)
        w1_wd = [deal_w1(b) for b in range(halves)]

        v_w = []
        for a in range(2):
            words = held("v_w%d" % a, [PART, S], U32)
            nc.vector.tensor_copy(words[:], tab_w[a][:].indirect(idx[:]))
            v_w.append(words)
        w4_grouped = []
        for b in range(halves):
            grouped = ring.tile([PART, PACK * BANK], BF16, name="grouped", tag="grouped", align_bytes=64)
            for u in range(2):
                nc.scalar.copy(
                    grouped[:, u * 2 * BANK : (u + 1) * 2 * BANK].rearrange("p (c e i) -> p c i e", e=RUN, i=PACK),
                    w4_raw[b][:, :, u * BANK // 2 : (u + 1) * BANK // 2].rearrange("p i (c e) -> p c i e", e=RUN),
                )
            w4_grouped.append(grouped)
        w4q = []

        out_rows = out.rearrange("(g p) j -> p g j", p=PART)
        bank_tags = ["free0", "free1", "free2", "free3", "free4", "arg", "lin", "total"]

        def next_bank(per_bank, width):
            tag = bank_tags.pop(0)
            bank_tags.append(tag)
            return psum.tile([PART, per_bank, width], F32, name="bank", tag=tag, bufs=1)

        def make_z(b, c0, width, z, copy):
            cols = slice(c0, c0 + width)
            per_bank = BANK // width
            for t0 in range(0, PACK, per_bank):
                img = next_bank(per_bank, width)
                for u in range(per_bank):
                    r0 = PART * (t0 + u)
                    for a in range(2):
                        nc.tensor.matmul_mx(
                            out=img[:, u, :], lhsT=w1_wd[b][:, a, 2 * r0 : 2 * (r0 + PART)].bitcast(FP4X4),
                            lhsT_scale=w1_sd[a][:, PASS * b + r0 : PASS * b + r0 + PART],
                            rhs=v_w[a][:, cols].bitcast(FP8X4), rhs_scale=v_s[a][:, cols],
                            start=(a == 0), stop=(a == 1),
                        )
                for u in range(per_bank):
                    t = t0 + u
                    nc.vector.scalar_tensor_tensor(
                        z[:, t, :], img[:, u, :], caps[:, b, t : t + 1], gate[PACK * b + t][:, cols], ALU.min, ALU.add
                    )
            regrouped = ring.tile([PART, PACK * width], BF16, name="zg", tag="zg%d" % b, bufs=2 + b, align_bytes=64)
            piece = min(width, CHUNKS[0])
            for j0 in range(0, width, piece):
                copy(
                    regrouped[:, PACK * j0 : PACK * (j0 + piece)].rearrange("p (c e t) -> p c t e", e=RUN, t=PACK),
                    z[:, :, j0 : j0 + piece].rearrange("p t (c e) -> p c t e", e=RUN),
                )
            return regrouped

        first_regrouped = []
        zq_first = []

        def finish(c0, width, regrouped):
            codes, scales = zq_first[c0 // BANK]
            inner = slice(c0 % BANK, c0 % BANK + width)
            second = quantised("zq_second%d" % c0, regrouped[:], width)
            zq = [(codes[:, inner], scales[:, inner]), (second[0][:], second[1][:])]
            per_bank = BANK // width
            staged = shared.tile([PART, N // PART, width], F32, name="staged%d" % c0, offset=4 * (N // PART) * c0)
            for g0 in range(0, N // PART, per_bank):
                acc = next_bank(per_bank, width)
                for u in range(per_bank):
                    rows = slice(PART * (g0 + u), PART * (g0 + u + 1))
                    for b in range(halves):
                        nc.tensor.matmul_mx(
                            out=acc[:, u, :], lhsT=w4q[b][0][:, rows].bitcast(FP8X4), lhsT_scale=w4q[b][1][:, rows],
                            rhs=zq[b][0].bitcast(FP8X4), rhs_scale=zq[b][1],
                            start=(b == 0), stop=(b == halves - 1),
                        )
                nc.scalar.copy(staged[:, g0 : g0 + per_bank, :], acc[:])
            nc.sync.dma_start(out=out_rows[:, :, c0 : c0 + width], in_=staged[:])

        starts = [sum(CHUNKS[:i]) for i in range(len(CHUNKS))]
        waiting = None
        for c0, width in zip(starts, CHUNKS):
            if c0 % BANK == 0:
                z_first = ring.tile([PART, PACK, BANK], BF16, name="z", tag="z_first")
                first_regrouped.append(make_z(0, c0, BANK, z_first, nc.scalar.copy))
            z_second = shared.tile([PART, PACK, width], BF16, name="z_second%d" % c0, offset=SECOND_AT + 2 * PACK * c0)
            regrouped = make_z(1, c0, width, z_second, nc.vector.tensor_copy if c0 >= starts[-NARROW] else nc.scalar.copy)
            if c0 == 0:
                w4q.extend(quantised("w4q%d" % b, w4_grouped[b][:], N) for b in range(halves))
            if c0 % BANK == 0:
                zq_first.append(quantised("zq_first%d" % c0, first_regrouped[c0 // BANK][:], BANK))
            if waiting is not None:
                finish(*waiting)
            waiting = (c0, width, regrouped)
            if c0 == 0:
                finish(*waiting)
                waiting = None
        finish(*waiting)
